import numpy as np
import ml_dtypes


def mxq(x, axis, fmt="e4m3"):
    dtype, down = {"e4m3": (ml_dtypes.float8_e4m3fn, 7), "e5m2": (ml_dtypes.float8_e5m2, 14)}[fmt]
    v = np.moveaxis(np.asarray(x, np.float32).astype(ml_dtypes.bfloat16).astype(np.float64), axis, -1)
    blocks = v.reshape(v.shape[:-1] + (-1, 32))
    amax = np.abs(blocks).max(-1, keepdims=True)
    byte = np.maximum(np.where(amax > 0, np.frexp(amax)[1] - 1 + 127, 0) - down, 1)
    scale = np.exp2(byte - 127.0)
    codes = (blocks / scale).astype(np.float32).astype(dtype).astype(np.float64)
    return np.moveaxis((codes * scale).reshape(v.shape), -1, axis)


WIDE = False


def mx_kscale(k):
    if not WIDE:
        return np.ones(k)
    levels = np.array([10, -10, 5, -5, 0])
    if k % 512:
        return np.exp2(np.random.permutation(np.resize(levels, k // 32))).repeat(32)
    a = np.empty((k // 512, 16))
    for p in range(k // 512):
        a[p, :8] = np.random.permutation(np.resize(levels, 8))
        for g in range(8):
            far = levels[np.abs(levels - a[p, g]) >= 10]
            a[p, g + 8] = far[np.random.randint(len(far))]
    return np.exp2(a.ravel()).repeat(32)


def f64(x):
    return np.asarray(x).astype(np.float64)


def striped(idx):
    return np.tile(idx.reshape(-1, 16).T, (8, 1)).astype(np.uint16)


def unstriped(offs):
    return offs[:16].T.reshape(-1).astype(np.int64)


def pack_weight(w):
    k, n = w.shape
    w = f64(np.asarray(w, np.float32).astype(ml_dtypes.bfloat16)).reshape(k // 32, 32, n)
    amax = np.abs(w).max(1)
    byte = np.clip(np.where(amax > 0, np.frexp(amax)[1] - 1 + 127 - 7, 1), 1, 254)
    scaled = (w * np.exp2(127.0 - byte)[:, None, :]).reshape(k, n).astype(np.float32)
    words = np.ascontiguousarray(scaled.reshape(k // 512, 128, 4, n).transpose(0, 1, 3, 2)).astype(ml_dtypes.float8_e4m3fn).view(np.uint8)
    return words, np.ascontiguousarray(byte.astype(np.uint8).reshape(k // 512, 16, n))


def unpack_weight(words, scales):
    g, p, n, _ = words.shape
    vals = np.ascontiguousarray(words).view(ml_dtypes.float8_e4m3fn).astype(np.float64) * np.repeat(np.exp2(scales.astype(np.float64) - 127.0), 8, axis=1)[..., None]
    return vals.transpose(0, 1, 3, 2).reshape(g * 512, n)


def silu(v):
    return v / (1.0 + np.exp(-np.maximum(v, -700.0)))


K, T, S, D, V, H, N = 1024, 2048, 1024, 3, 512, 512, 128
P = 2 ** 7


def setup_inputs():
    n = np.random.standard_normal
    s = mx_kscale(K)[:, None]
    u = mx_kscale(H)
    packed_xT = pack_weight(n((K, T)) * s)
    packed_w2 = pack_weight(n((H, N)) / np.sqrt(H) / u[:, None])
    return {
        "x_words": packed_xT[0],
        "x_scales": packed_xT[1],
        "w1": (n((K, H)) / np.sqrt(K) / s * u).astype(np.float32),
        "w2_words": packed_w2[0],
        "w2_scales": packed_w2[1],
        "gate": (np.tile(np.random.uniform(0.2, 1.0, (D, 1, V)) / np.sqrt(D), (1, P, 1))).astype(np.float32),
        "offs": striped(np.random.permutation(T)[:S]),
        "cen": striped(np.random.permutation(S)[:V]),
        "pos1": striped(np.random.permutation(S)[:V]),
        "pos2": striped(np.random.permutation(S)[:V]),
        "pos3": striped(np.random.permutation(S)[:V]),
    }


def reference(x_words, x_scales, w1, w2_words, w2_scales, gate, offs, cen, pos1, pos2, pos3):
    xq = unpack_weight(x_words, x_scales)[:, unstriped(offs)]
    h = silu(mxq(f64(w1), 0, "e4m3").T @ xq)
    z = h[:, unstriped(cen)] - (h[:, unstriped(pos1)] * f64(gate)[0, :1] + h[:, unstriped(pos2)] * f64(gate)[1, :1] + h[:, unstriped(pos3)] * f64(gate)[2, :1])
    return unpack_weight(w2_words, w2_scales).T @ mxq(z, 0, "e4m3")

@@ -1,0 +1,269 @@
+from contextlib import ExitStack
+
+import concourse.mybir as mybir
+from concourse.masks import make_identity
+
+K, T, S, D, V, H, N = 1024, 2048, 1024, 3, 512, 512, 128
+FLOPS = 2 * K * H * S + 2 * H * N * V
+
+F32 = mybir.dt.float32
+BF16 = mybir.dt.bfloat16
+I32 = mybir.dt.int32
+U32 = mybir.dt.uint32
+U16 = mybir.dt.uint16
+U8 = mybir.dt.uint8
+FP8X4 = mybir.dt.float8_e4m3fn_x4
+ACT = mybir.ActivationFunctionType
+MULT = mybir.AluOpType.mult
+SUBTRACT = mybir.AluOpType.subtract
+
+P = 128
+PACK = 4
+PASSES = K // (P * PACK)
+H_TILES = H // P
+V_BLOCKS = V // P
+BANK = 512
+STRIPE = 16
+QUADS = 4
+QUAD = 32
+
+
+def tile_picked_lapl_silu_p_kernel(
+    tc, x_words, x_scales, w1, w2_words, w2_scales, gate, offs, cen, pos1, pos2, pos3, out
+):
+    nc = tc.nc
+    with ExitStack() as ctx:
+        keep = ctx.enter_context(tc.tile_pool(name="keep", bufs=1))
+        psum = ctx.enter_context(tc.psum_pool(name="psum", bufs=1))
+
+        def bank(n, name):
+            return psum.tile([P, BANK], F32, name=name, tag="bank%d" % n)
+
+        def load_list(source, name):
+            tile = keep.tile(list(source.shape), U16, name=name)
+            nc.sync.dma_start(tile[:], source)
+            return tile
+
+        def load_words(z):
+            tile = keep.tile([P, T], I32, name="x_window%d" % z)
+            nc.sync.dma_start(out=tile[:], in_=x_words[z].rearrange("p n j -> p (n j)").bitcast(I32))
+            return tile
+
+        def load_w1(t, z):
+            tile = keep.tile([P, PACK, P], F32, name="w1_raw%d_%d" % (t, z))
+            rows = w1[z * P * PACK : (z + 1) * P * PACK, t * P : (t + 1) * P]
+            nc.sync.dma_start(out=tile[:], in_=rows.rearrange("(p j) c -> p j c", j=PACK))
+            return tile
+
+        def load_w1_block(t):
+            tile = keep.tile([P, PASSES, PACK, P], F32, name="w1_block%d" % t)
+            for z in range(PASSES):
+                rows = w1[z * P * PACK : (z + 1) * P * PACK, t * P : (t + 1) * P]
+                nc.sync.dma_start(out=tile[:, z], in_=rows.rearrange("(p j) c -> p j c", j=PACK))
+            return tile
+
+        def load_gate(d):
+            tile = keep.tile([P, V], F32, name="gate%d" % d)
+            nc.sync.dma_start(out=tile[:], in_=gate[d])
+            return tile
+
+        scale_window = keep.tile([P, T], U8, name="scale_window")
+        nc.vector.memset(scale_window[:].bitcast(I32), 0)
+        warm = keep.tile([P, 2], F32, name="warm")
+        nc.vector.memset(warm[:, 0:1], 0.0)
+        nc.scalar.activation(out=warm[:, 1:2], in_=warm[:, 0:1], func=ACT.Silu)
+
+        offs_t = load_list(offs, "offs_t")
+        for q in range(QUADS):
+            nc.sync.dma_start(
+                out=scale_window[QUAD * q : QUAD * q + PASSES * PACK, :].bitcast(I32),
+                in_=x_scales[:, PACK * q : PACK * (q + 1), :].bitcast(I32),
+            )
+        x_window = [load_words(0)]
+        w1_raw = {(0, 0): load_w1(0, 0)}
+        x_window.append(load_words(1))
+        w1_raw[0, 1] = load_w1(0, 1)
+        w1_block = {1: load_w1_block(1)}
+        gates = []
+        pos_t = []
+        for d, source in enumerate((pos1, pos2, pos3)):
+            pos_t.append(load_list(source, "pos_t%d" % d))
+            gates.append(load_gate(d))
+        cen_t = load_list(cen, "cen_t")
+        for t in range(2, H_TILES):
+            w1_block[t] = load_w1_block(t)
+        w2_codes = keep.tile([P, N], I32, name="w2_codes", align_bytes=64)
+        nc.sync.dma_start(out=w2_codes[:], in_=w2_words[0].rearrange("p n j -> p (n j)").bitcast(I32))
+        w2_plane = keep.tile([P, N], U8, name="w2_plane", align_bytes=64)
+        nc.gpsimd.memset(w2_plane[:].bitcast(I32), 0)
+        for q in range(QUADS):
+            nc.sync.dma_start(
+                out=w2_plane[QUAD * q : QUAD * q + PACK, :].bitcast(I32),
+                in_=w2_scales[0, PACK * q : PACK * (q + 1), :].bitcast(I32),
+            )
+
+        ident = keep.tile([P, P], F32, name="ident")
+        make_identity(nc, ident[:])
+
+        def quantize_w1(t, z):
+            grouped = keep.tile([P, P, PACK], BF16, name="w1_bf%d_%d" % (t, z), align_bytes=64)
+            nc.scalar.copy(
+                out=grouped[:].rearrange("p (c i) j -> p c j i", i=PACK),
+                in_=w1_raw[t, z][:].rearrange("p j (c i) -> p c j i", i=PACK),
+            )
+            codes = keep.tile([P, P], U32, name="w1_codes%d_%d" % (t, z), align_bytes=64)
+            plane = keep.tile([P, P], U8, name="w1_plane%d_%d" % (t, z), align_bytes=64)
+            nc.vector.quantize_mx(
+                out=codes[:].bitcast(FP8X4), scales=plane[:], in_=grouped[:].rearrange("p c j -> p (c j)")
+            )
+            return codes[:], plane[:]
+
+        def quantize_w1_block(t):
+            grouped = keep.tile(
+                [P, PASSES, P, PACK], BF16, name="w1_bf%d" % t, tag="staging%d" % t, align_bytes=64
+            )
+            cast = nc.vector.tensor_copy if t == 1 else nc.scalar.copy
+            cast(
+                out=grouped[:].rearrange("p z (c i) j -> p z c j i", i=PACK),
+                in_=w1_block[t][:].rearrange("p z j (c i) -> p z c j i", i=PACK),
+            )
+            codes = keep.tile([P, PASSES, P], U32, name="w1_codes%d" % t, align_bytes=64)
+            plane = keep.tile([P, PASSES, P], U8, name="w1_plane%d" % t, align_bytes=64)
+            nc.vector.quantize_mx(
+                out=codes[:].rearrange("p z c -> p (z c)").bitcast(FP8X4),
+                scales=plane[:].rearrange("p z c -> p (z c)"),
+                in_=grouped[:].rearrange("p z c j -> p (z c j)"),
+            )
+            for z in range(PASSES):
+                w1_mx[t, z] = (codes[:, z, :], plane[:, z, :])
+
+        x_plane = keep.tile([P, S], U8, name="x_plane", align_bytes=64)
+        x_codes = [keep.tile([P, S], U32, name="x_codes%d" % z, align_bytes=64) for z in range(PASSES)]
+
+        def pick(dst, window, a, b):
+            nc.vector.tensor_copy(dst[:, a:b], window.indirect(offs_t[:, a // STRIPE : b // STRIPE]))
+
+        pick(x_plane, scale_window[:], 0, S)
+        pick(x_codes[0], x_window[0][:].bitcast(U32), 0, S)
+        w1_mx = {(0, 0): quantize_w1(0, 0), (0, 1): quantize_w1(0, 1)}
+        first_pieces = [(0, 512), (512, 768), (768, 1024)]
+        for a, b in first_pieces:
+            pick(x_codes[1], x_window[1][:].bitcast(U32), a, b)
+
+        def project(t, pieces, banks):
+            h = keep.tile([P, S], F32, name="h%d" % t)
+            for (a, b), n in zip(pieces, banks):
+                acc = bank(n, "acc")
+                for z in range(PASSES):
+                    codes, plane = w1_mx[t, z]
+                    nc.tensor.matmul_mx(
+                        out=acc[:, 0 : b - a],
+                        lhsT=codes.bitcast(FP8X4),
+                        lhsT_scale=plane,
+                        rhs=x_codes[z][:, a:b].bitcast(FP8X4),
+                        rhs_scale=x_plane[PACK * z : P, a:b],
+                        start=(z == 0),
+                        stop=(z == PASSES - 1),
+                    )
+                nc.scalar.activation(out=h[:, a:b], in_=acc[:, 0 : b - a], func=ACT.Silu)
+            return h
+
+        quantize_w1_block(1)
+        h_tiles = [project(0, first_pieces, (0, 1, 2))]
+        signed_gates = [gates[0]]
+        for d in range(1, D):
+            tile = keep.tile([P, V], F32, name="minus_gate%d" % d)
+            nc.scalar.mul(out=tile[:], in_=gates[d][:], mul=-1.0)
+            signed_gates.append(tile)
+
+        z_bf = [keep.tile([P, 2, P, 2], BF16, name="z_bf%d" % vb) for vb in range(V_BLOCKS)]
+        slot_of = {(0, 0, 0): "staging1", (1, 1, 0): "staging2", (1, 2, 0): "staging3", (3, 0, 3 * P): "z_words0", (3, 2, 3 * P): "z_words1"}
+
+        def fetch_terms(t, a, b, each):
+            cols = slice(a // STRIPE, b // STRIPE)
+            first = None
+            order = (0, D, 1, 2) if t == 0 else (0, 1, 2, D)
+            for n in order:
+                tag = slot_of.get((t, n, a), "term%d_%d_%d" % (t, n, a))
+                term = keep.tile([P, b - a], F32, name="term", tag=tag, align_bytes=64)
+                if n < D:
+                    nc.vector.tensor_tensor(
+                        term[:], h_tiles[t][:].indirect(pos_t[n][:, cols]), signed_gates[n][:, a:b], MULT
+                    )
+                else:
+                    nc.vector.tensor_tensor(term[:], h_tiles[t][:].indirect(cen_t[:, cols]), first[:], SUBTRACT)
+                if n == 0:
+                    first = term
+                else:
+                    each(n, term)
+
+        def add_turned(dst, src, n):
+            nc.tensor.matmul(dst, lhsT=src, rhs=ident[:], is_transpose=True, start=(n == 1), stop=(n == D))
+
+        def round_block(t, vb, src):
+            nc.scalar.copy(
+                out=z_bf[vb][:, :, QUAD * t : QUAD * (t + 1), :],
+                in_=src.rearrange("v (m u e) -> v u m e", u=2, e=2),
+            )
+
+        def sum_late(t, n_bank):
+            terms = {}
+            fetch_terms(t, 0, V, terms.setdefault)
+            total = bank(n_bank, "z_sum")
+            for vb in range(V_BLOCKS):
+                for n in range(1, D + 1):
+                    add_turned(total[:, vb * P : (vb + 1) * P], terms[n][:, vb * P : (vb + 1) * P], n)
+            for vb in range(V_BLOCKS):
+                round_block(t, vb, total[:, vb * P : (vb + 1) * P])
+
+        def sum_at_once(t, blocks, first_bank):
+            a = blocks[0] * P
+            banks = {vb: bank(first_bank + vb, "z_sum") for vb in blocks}
+
+            def each(n, term):
+                for vb in blocks:
+                    add_turned(banks[vb][:, 0:P], term[:, vb * P - a : (vb + 1) * P - a], n)
+
+            fetch_terms(t, a, (blocks[-1] + 1) * P, each)
+            for vb in blocks:
+                round_block(t, vb, banks[vb][:, 0:P])
+
+        def second_layer(vb):
+            words = z_bf[vb][:].rearrange("v u m e -> v (u m e)").bitcast(F32)
+            turned = bank(vb, "turned")
+            for u in range(2):
+                nc.tensor.transpose(turned[:, u * P : (u + 1) * P], words[:, u * P : (u + 1) * P], ident[:])
+            grouped = keep.tile([P, P, 2], F32, name="z_grouped", tag="z_words%d" % vb, align_bytes=64)
+            nc.scalar.copy(out=grouped[:], in_=turned[:, 0 : 2 * P].rearrange("m (u v) -> m v u", u=2))
+            codes = keep.tile([P, P], U32, name="z_codes%d" % vb, align_bytes=64)
+            plane = keep.tile([P, P], U8, name="z_plane%d" % vb, align_bytes=64)
+            nc.vector.quantize_mx(
+                out=codes[:].bitcast(FP8X4),
+                scales=plane[:],
+                in_=grouped[:].rearrange("m v u -> m (v u)").bitcast(BF16),
+            )
+            acc = bank(vb, "out_acc")
+            nc.tensor.matmul_mx(
+                out=acc[:, 0:P],
+                lhsT=w2_codes[:].bitcast(FP8X4),
+                lhsT_scale=w2_plane[:],
+                rhs=codes[:].bitcast(FP8X4),
+                rhs_scale=plane[:],
+                start=True,
+                stop=True,
+            )
+            result = keep.tile([P, P], F32, name="result%d" % vb)
+            nc.scalar.copy(out=result[:], in_=acc[:, 0:P])
+            nc.sync.dma_start(out=out[:, vb * P : (vb + 1) * P], in_=result[:])
+
+        halves = [(0, BANK), (BANK, S)]
+        h_tiles.append(project(1, halves, (3, 4)))
+        for t, banks in ((2, (5, 6)), (3, (0, 7))):
+            quantize_w1_block(t)
+            h_tiles.append(project(t, halves, banks))
+        sum_late(0, 6)
+        sum_late(1, 7)
+        sum_at_once(2, list(range(V_BLOCKS)), 0)
+        for vb in range(V_BLOCKS):
+            sum_at_once(3, [vb], 4)
+            second_layer(vb)

@@ -56,7 +56,7 @@ def tile_picked_lapl_silu_p_kernel(
             return tile
 
         def load_w1_block(t):
-            tile = keep.tile([P, PASSES, PACK, P], F32, name="w1_block%d" % t)
+            tile = keep.tile([P, PASSES, PACK, P], F32, name="w1_block", tag="w1_block%d" % t)
             for z in range(PASSES):
                 rows = w1[z * P * PACK : (z + 1) * P * PACK, t * P : (t + 1) * P]
                 nc.sync.dma_start(out=tile[:, z], in_=rows.rearrange("(p j) c -> p j c", j=PACK))
@@ -69,20 +69,16 @@ def tile_picked_lapl_silu_p_kernel(
 
         scale_window = keep.tile([P, T], U8, name="scale_window")
         nc.vector.memset(scale_window[:].bitcast(I32), 0)
-        warm = keep.tile([P, 2], F32, name="warm")
-        nc.vector.memset(warm[:, 0:1], 0.0)
-        nc.scalar.activation(out=warm[:, 1:2], in_=warm[:, 0:1], func=ACT.Silu)
 
+        x_window = [load_words(0)]
         offs_t = load_list(offs, "offs_t")
         for q in range(QUADS):
             nc.sync.dma_start(
                 out=scale_window[QUAD * q : QUAD * q + PASSES * PACK, :].bitcast(I32),
                 in_=x_scales[:, PACK * q : PACK * (q + 1), :].bitcast(I32),
             )
-        x_window = [load_words(0)]
-        w1_raw = {(0, 0): load_w1(0, 0)}
+        w1_raw = {(0, z): load_w1(0, z) for z in range(PASSES)}
         x_window.append(load_words(1))
-        w1_raw[0, 1] = load_w1(0, 1)
         w1_block = {1: load_w1_block(1)}
         gates = []
         pos_t = []
@@ -122,8 +118,7 @@ def tile_picked_lapl_silu_p_kernel(
             grouped = keep.tile(
                 [P, PASSES, P, PACK], BF16, name="w1_bf%d" % t, tag="staging%d" % t, align_bytes=64
             )
-            cast = nc.vector.tensor_copy if t == 1 else nc.scalar.copy
-            cast(
+            nc.scalar.copy(
                 out=grouped[:].rearrange("p z (c i) j -> p z c j i", i=PACK),
                 in_=w1_block[t][:].rearrange("p z j (c i) -> p z c j i", i=PACK),
             )
@@ -151,7 +146,7 @@ def tile_picked_lapl_silu_p_kernel(
             pick(x_codes[1], x_window[1][:].bitcast(U32), a, b)
 
         def project(t, pieces, banks):
-            h = keep.tile([P, S], F32, name="h%d" % t)
+            h = keep.tile([P, S], F32, name="h", tag="w1_block1" if t == 0 else "h%d" % t)
             for (a, b), n in zip(pieces, banks):
                 acc = bank(n, "acc")
                 for z in range(PASSES):
@@ -177,7 +172,7 @@ def tile_picked_lapl_silu_p_kernel(
             signed_gates.append(tile)
 
         z_bf = [keep.tile([P, 2, P, 2], BF16, name="z_bf%d" % vb) for vb in range(V_BLOCKS)]
-        slot_of = {(0, 0, 0): "staging1", (1, 1, 0): "staging2", (1, 2, 0): "staging3", (3, 0, 3 * P): "z_words0", (3, 2, 3 * P): "z_words1"}
+        slot_of = {(0, 0, 0): "staging1", (1, 0, 0): "staging2", (1, 1, 0): "staging3"}
 
         def fetch_terms(t, a, b, each):
             cols = slice(a // STRIPE, b // STRIPE)
@@ -216,9 +211,9 @@ def tile_picked_lapl_silu_p_kernel(
             for vb in range(V_BLOCKS):
                 round_block(t, vb, total[:, vb * P : (vb + 1) * P])
 
-        def sum_at_once(t, blocks, first_bank):
+        def sum_at_once(t, blocks, bank_numbers):
             a = blocks[0] * P
-            banks = {vb: bank(first_bank + vb, "z_sum") for vb in blocks}
+            banks = {vb: bank(n, "z_sum") for vb, n in zip(blocks, bank_numbers)}
 
             def each(n, term):
                 for vb in blocks:
@@ -228,33 +223,42 @@ def tile_picked_lapl_silu_p_kernel(
             for vb in blocks:
                 round_block(t, vb, banks[vb][:, 0:P])
 
-        def second_layer(vb):
-            words = z_bf[vb][:].rearrange("v u m e -> v (u m e)").bitcast(F32)
-            turned = bank(vb, "turned")
-            for u in range(2):
-                nc.tensor.transpose(turned[:, u * P : (u + 1) * P], words[:, u * P : (u + 1) * P], ident[:])
-            grouped = keep.tile([P, P, 2], F32, name="z_grouped", tag="z_words%d" % vb, align_bytes=64)
-            nc.scalar.copy(out=grouped[:], in_=turned[:, 0 : 2 * P].rearrange("m (u v) -> m v u", u=2))
-            codes = keep.tile([P, P], U32, name="z_codes%d" % vb, align_bytes=64)
-            plane = keep.tile([P, P], U8, name="z_plane%d" % vb, align_bytes=64)
+        def turn_back(blocks, turn_bank):
+            first, width = blocks[0], len(blocks) * P
+            turned = bank(turn_bank, "turned")
+            for i, vb in enumerate(blocks):
+                words = z_bf[vb][:].rearrange("v u m e -> v (u m e)").bitcast(F32)
+                for u in range(2):
+                    at = u * width + i * P
+                    nc.tensor.transpose(turned[:, at : at + P], words[:, u * P : (u + 1) * P], ident[:])
+            grouped = keep.tile([P, width, 2], F32, name="z_grouped", tag="z_words%d" % first, align_bytes=64)
+            nc.scalar.copy(out=grouped[:], in_=turned[:, 0 : 2 * width].rearrange("m (u v) -> m v u", u=2))
+            codes = keep.tile([P, width], U32, name="z_codes%d" % first, align_bytes=64)
+            plane = keep.tile([P, width], U8, name="z_plane%d" % first, align_bytes=64)
             nc.vector.quantize_mx(
                 out=codes[:].bitcast(FP8X4),
                 scales=plane[:],
                 in_=grouped[:].rearrange("m v u -> m (v u)").bitcast(BF16),
             )
-            acc = bank(vb, "out_acc")
-            nc.tensor.matmul_mx(
-                out=acc[:, 0:P],
-                lhsT=w2_codes[:].bitcast(FP8X4),
-                lhsT_scale=w2_plane[:],
-                rhs=codes[:].bitcast(FP8X4),
-                rhs_scale=plane[:],
-                start=True,
-                stop=True,
-            )
-            result = keep.tile([P, P], F32, name="result%d" % vb)
-            nc.scalar.copy(out=result[:], in_=acc[:, 0:P])
-            nc.sync.dma_start(out=out[:, vb * P : (vb + 1) * P], in_=result[:])
+            return first * P, codes, plane
+
+        def project_out(groups, leave, out_bank):
+            first = groups[0][0]
+            acc = bank(out_bank, "out_acc")
+            for start, codes, plane in groups:
+                end = start - first + codes.shape[1]
+                nc.tensor.matmul_mx(
+                    out=acc[:, start - first : end],
+                    lhsT=w2_codes[:].bitcast(FP8X4),
+                    lhsT_scale=w2_plane[:],
+                    rhs=codes[:].bitcast(FP8X4),
+                    rhs_scale=plane[:],
+                    start=True,
+                    stop=True,
+                )
+            result = keep.tile([P, end], F32, name="result%d" % first)
+            leave(out=result[:], in_=acc[:, 0:end])
+            nc.sync.dma_start(out=out[:, first : first + end], in_=result[:])
 
         halves = [(0, BANK), (BANK, S)]
         h_tiles.append(project(1, halves, (3, 4)))
@@ -263,7 +267,13 @@ def tile_picked_lapl_silu_p_kernel(
             h_tiles.append(project(t, halves, banks))
         sum_late(0, 6)
         sum_late(1, 7)
-        sum_at_once(2, list(range(V_BLOCKS)), 0)
-        for vb in range(V_BLOCKS):
-            sum_at_once(3, [vb], 4)
-            second_layer(vb)
+        sum_at_once(2, [0, 1, 2], [0, 1, 2])
+        sum_at_once(3, [0, 1], [3, 4])
+        early = [turn_back([0, 1], 6)]
+        sum_at_once(3, [2], [4])
+        sum_at_once(2, [3], [6])
+        early.append(turn_back([2], 7))
+        sum_at_once(3, [3], [7])
+        last = turn_back([3], 0)
+        project_out(early, nc.scalar.copy, 7)
+        project_out([last], nc.vector.tensor_copy, 2)

@@ -69,6 +69,9 @@ def tile_picked_lapl_silu_p_kernel(
 
         scale_window = keep.tile([P, T], U8, name="scale_window")
         nc.vector.memset(scale_window[:].bitcast(I32), 0)
+        warm = keep.tile([P, 2], F32, name="warm")
+        nc.vector.memset(warm[:, 0:1], 0.0)
+        nc.scalar.activation(out=warm[:, 1:2], in_=warm[:, 0:1], func=ACT.Silu)
 
         x_window = [load_words(0)]
         offs_t = load_list(offs, "offs_t")
@@ -171,14 +174,13 @@ def tile_picked_lapl_silu_p_kernel(
             nc.scalar.mul(out=tile[:], in_=gates[d][:], mul=-1.0)
             signed_gates.append(tile)
 
-        z_bf = [keep.tile([P, 2, P, 2], BF16, name="z_bf%d" % vb) for vb in range(V_BLOCKS)]
+        z_bf = [keep.tile([P, 2, P, 2], BF16, name="z_bf", tag="w1_block3" if vb == 0 else "z_bf%d" % vb) for vb in range(V_BLOCKS)]
         slot_of = {(0, 0, 0): "staging1", (1, 0, 0): "staging2", (1, 1, 0): "staging3"}
 
         def fetch_terms(t, a, b, each):
             cols = slice(a // STRIPE, b // STRIPE)
             first = None
-            order = (0, D, 1, 2) if t == 0 else (0, 1, 2, D)
-            for n in order:
+            for n in range(D + 1):
                 tag = slot_of.get((t, n, a), "term%d_%d_%d" % (t, n, a))
                 term = keep.tile([P, b - a], F32, name="term", tag=tag, align_bytes=64)
                 if n < D:
@@ -262,15 +264,15 @@ def tile_picked_lapl_silu_p_kernel(
 
         halves = [(0, BANK), (BANK, S)]
         h_tiles.append(project(1, halves, (3, 4)))
-        for t, banks in ((2, (5, 6)), (3, (0, 7))):
+        for t, banks in ((2, (1, 2)), (3, (3, 4))):
             quantize_w1_block(t)
             h_tiles.append(project(t, halves, banks))
-        sum_late(0, 6)
-        sum_late(1, 7)
+        sum_at_once(0, [0, 1, 2, 3], [5, 6, 7, 0])
+        sum_late(1, 4)
         sum_at_once(2, [0, 1, 2], [0, 1, 2])
-        sum_at_once(3, [0, 1], [3, 4])
+        sum_at_once(3, [0, 1], [3, 5])
         early = [turn_back([0, 1], 6)]
-        sum_at_once(3, [2], [4])
+        sum_at_once(3, [2], [5])
         sum_at_once(2, [3], [6])
         early.append(turn_back([2], 7))
         sum_at_once(3, [3], [7])

@@ -26,6 +26,15 @@ BANK = 512
 STRIPE = 16
 QUADS = 4
 QUAD = 32
+LAST = 256
+PLACES = {
+    "term1_0_0": 0,
+    "w1_raw2": 1024,
+    "term1_1_0": 2048,
+    "term1_2_0": 5120,
+    "w1_raw3": 6144,
+    "h2": 7168,
+}
 
 
 def tile_picked_lapl_silu_p_kernel(
@@ -33,67 +42,65 @@ def tile_picked_lapl_silu_p_kernel(
 ):
     nc = tc.nc
     with ExitStack() as ctx:
+        lists = ctx.enter_context(tc.tile_pool(name="lists", bufs=1))
         keep = ctx.enter_context(tc.tile_pool(name="keep", bufs=1))
+        shared = ctx.enter_context(tc.tile_pool(name="shared", bufs=1))
         psum = ctx.enter_context(tc.psum_pool(name="psum", bufs=1))
+
+        def sbuf(shape, dtype, name, tag=None):
+            if name in PLACES:
+                return shared.tile(shape, dtype, name=name, align_bytes=64, offset=PLACES[name])
+            return keep.tile(shape, dtype, name=name, tag=tag or name, align_bytes=64)
 
         def bank(n, name):
             return psum.tile([P, BANK], F32, name=name, tag="bank%d" % n)
 
         def load_list(source, name):
-            tile = keep.tile(list(source.shape), U16, name=name)
+            tile = lists.tile(list(source.shape), U16, name=name)
             nc.sync.dma_start(tile[:], source)
             return tile
 
         def load_words(z):
-            tile = keep.tile([P, T], I32, name="x_window%d" % z)
+            tile = sbuf([P, T], I32, "x_window%d" % z)
             nc.sync.dma_start(out=tile[:], in_=x_words[z].rearrange("p n j -> p (n j)").bitcast(I32))
             return tile
 
-        def load_w1(t, z):
-            tile = keep.tile([P, PACK, P], F32, name="w1_raw%d_%d" % (t, z))
-            rows = w1[z * P * PACK : (z + 1) * P * PACK, t * P : (t + 1) * P]
-            nc.sync.dma_start(out=tile[:], in_=rows.rearrange("(p j) c -> p j c", j=PACK))
-            return tile
-
-        def load_w1_block(t):
-            tile = keep.tile([P, PASSES, PACK, P], F32, name="w1_block", tag="w1_block%d" % t)
-            for z in range(PASSES):
+        def load_w1(t, passes):
+            name = "w1_raw%d" % t if len(passes) == PASSES else "w1_raw%d_%d" % (t, passes[0])
+            tile = sbuf([P, len(passes), PACK, P], F32, name)
+            for i, z in enumerate(passes):
                 rows = w1[z * P * PACK : (z + 1) * P * PACK, t * P : (t + 1) * P]
-                nc.sync.dma_start(out=tile[:, z], in_=rows.rearrange("(p j) c -> p j c", j=PACK))
+                nc.sync.dma_start(out=tile[:, i], in_=rows.rearrange("(p j) c -> p j c", j=PACK))
             return tile
 
-        def load_gate(d):
-            tile = keep.tile([P, V], F32, name="gate%d" % d)
-            nc.sync.dma_start(out=tile[:], in_=gate[d])
-            return tile
-
-        scale_window = keep.tile([P, T], U8, name="scale_window")
-        nc.vector.memset(scale_window[:].bitcast(I32), 0)
-        warm = keep.tile([P, 2], F32, name="warm")
+        scale_window = sbuf([P, T], U8, "scale_window")
+        nc.gpsimd.memset(scale_window[:].bitcast(I32), 0)
+        warm = sbuf([P, 2], F32, "warm")
         nc.vector.memset(warm[:, 0:1], 0.0)
         nc.scalar.activation(out=warm[:, 1:2], in_=warm[:, 0:1], func=ACT.Silu)
 
-        x_window = [load_words(0)]
         offs_t = load_list(offs, "offs_t")
+        gate_row = sbuf([P, D, PACK], F32, "gate_row")
+        nc.sync.dma_start(out=gate_row[:], in_=gate[:, 0, :].rearrange("d (p j) -> p d j", j=PACK))
         for q in range(QUADS):
             nc.sync.dma_start(
                 out=scale_window[QUAD * q : QUAD * q + PASSES * PACK, :].bitcast(I32),
                 in_=x_scales[:, PACK * q : PACK * (q + 1), :].bitcast(I32),
             )
-        w1_raw = {(0, z): load_w1(0, z) for z in range(PASSES)}
-        x_window.append(load_words(1))
-        w1_block = {1: load_w1_block(1)}
-        gates = []
-        pos_t = []
-        for d, source in enumerate((pos1, pos2, pos3)):
-            pos_t.append(load_list(source, "pos_t%d" % d))
-            gates.append(load_gate(d))
+        x_window = []
+        w1_raw = {}
+        for z in range(PASSES):
+            x_window.append(load_words(z))
+            w1_raw[0, z] = load_w1(0, [z])
+        for z in range(PASSES):
+            w1_raw[1, z] = load_w1(1, [z])
+        pos_t = [load_list(source, "pos_t%d" % d) for d, source in enumerate((pos1, pos2, pos3))]
         cen_t = load_list(cen, "cen_t")
         for t in range(2, H_TILES):
-            w1_block[t] = load_w1_block(t)
-        w2_codes = keep.tile([P, N], I32, name="w2_codes", align_bytes=64)
+            w1_raw[t, 0] = load_w1(t, [0, 1])
+        w2_codes = sbuf([P, N], I32, "w2_codes")
         nc.sync.dma_start(out=w2_codes[:], in_=w2_words[0].rearrange("p n j -> p (n j)").bitcast(I32))
-        w2_plane = keep.tile([P, N], U8, name="w2_plane", align_bytes=64)
+        w2_plane = sbuf([P, N], U8, "w2_plane")
         nc.gpsimd.memset(w2_plane[:].bitcast(I32), 0)
         for q in range(QUADS):
             nc.sync.dma_start(
@@ -101,142 +108,135 @@ def tile_picked_lapl_silu_p_kernel(
                 in_=w2_scales[0, PACK * q : PACK * (q + 1), :].bitcast(I32),
             )
 
-        ident = keep.tile([P, P], F32, name="ident")
+        ident = sbuf([P, P], F32, "ident")
         make_identity(nc, ident[:])
 
-        def quantize_w1(t, z):
-            grouped = keep.tile([P, P, PACK], BF16, name="w1_bf%d_%d" % (t, z), align_bytes=64)
-            nc.scalar.copy(
-                out=grouped[:].rearrange("p (c i) j -> p c j i", i=PACK),
-                in_=w1_raw[t, z][:].rearrange("p j (c i) -> p c j i", i=PACK),
-            )
-            codes = keep.tile([P, P], U32, name="w1_codes%d_%d" % (t, z), align_bytes=64)
-            plane = keep.tile([P, P], U8, name="w1_plane%d_%d" % (t, z), align_bytes=64)
-            nc.vector.quantize_mx(
-                out=codes[:].bitcast(FP8X4), scales=plane[:], in_=grouped[:].rearrange("p c j -> p (c j)")
-            )
-            return codes[:], plane[:]
+        signed_gates = []
+        for d in range(D):
+            spread = bank(d, "gate_spread")
+            for j in range(PACK):
+                nc.tensor.transpose(
+                    spread[:, j * P : (j + 1) * P], gate_row[:, d, j : j + 1].to_broadcast([P, P]), ident[:]
+                )
+            tile = sbuf([P, P, PACK], F32, "signed_gate%d" % d)
+            nc.scalar.mul(out=tile[:], in_=spread[:].rearrange("p (j n) -> p n j", j=PACK), mul=1.0 if d == 0 else -1.0)
+            signed_gates.append(tile[:].rearrange("p n j -> p (n j)"))
 
-        def quantize_w1_block(t):
-            grouped = keep.tile(
-                [P, PASSES, P, PACK], BF16, name="w1_bf%d" % t, tag="staging%d" % t, align_bytes=64
-            )
+        w1_mx = {}
+
+        def quantize_w1(t, passes, staging_tag):
+            n = len(passes)
+            name = "%d_%d" % (t, passes[0])
+            grouped = sbuf([P, n, P, PACK], BF16, "w1_bf" + name, staging_tag)
             nc.scalar.copy(
                 out=grouped[:].rearrange("p z (c i) j -> p z c j i", i=PACK),
-                in_=w1_block[t][:].rearrange("p z j (c i) -> p z c j i", i=PACK),
+                in_=w1_raw[t, passes[0]][:].rearrange("p z j (c i) -> p z c j i", i=PACK),
             )
-            codes = keep.tile([P, PASSES, P], U32, name="w1_codes%d" % t, align_bytes=64)
-            plane = keep.tile([P, PASSES, P], U8, name="w1_plane%d" % t, align_bytes=64)
+            codes = sbuf([P, n * P], U32, "w1_codes" + name)
+            plane = sbuf([P, n * P], U8, "w1_plane" + name)
             nc.vector.quantize_mx(
-                out=codes[:].rearrange("p z c -> p (z c)").bitcast(FP8X4),
-                scales=plane[:].rearrange("p z c -> p (z c)"),
-                in_=grouped[:].rearrange("p z c j -> p (z c j)"),
+                out=codes[:].bitcast(FP8X4), scales=plane[:], in_=grouped[:].rearrange("p z c j -> p (z c j)")
             )
-            for z in range(PASSES):
-                w1_mx[t, z] = (codes[:, z, :], plane[:, z, :])
+            for i, z in enumerate(passes):
+                w1_mx[t, z] = (codes[:, i * P : (i + 1) * P], plane[:, i * P : (i + 1) * P])
 
-        x_plane = keep.tile([P, S], U8, name="x_plane", align_bytes=64)
-        x_codes = [keep.tile([P, S], U32, name="x_codes%d" % z, align_bytes=64) for z in range(PASSES)]
+        x_plane = sbuf([P, S], U8, "x_plane")
+        x_codes = [sbuf([P, S], U32, "x_codes0"), sbuf([P, S - LAST], U32, "x_codes1")]
 
         def pick(dst, window, a, b):
             nc.vector.tensor_copy(dst[:, a:b], window.indirect(offs_t[:, a // STRIPE : b // STRIPE]))
 
         pick(x_plane, scale_window[:], 0, S)
         pick(x_codes[0], x_window[0][:].bitcast(U32), 0, S)
-        w1_mx = {(0, 0): quantize_w1(0, 0), (0, 1): quantize_w1(0, 1)}
-        first_pieces = [(0, 512), (512, 768), (768, 1024)]
-        for a, b in first_pieces:
+        quantize_w1(0, [0], None)
+        for a, b in [(0, 512), (512, S - LAST)]:
             pick(x_codes[1], x_window[1][:].bitcast(U32), a, b)
+        quantize_w1(0, [1], None)
+        x_last = sbuf([P, LAST], U32, "x_last", "w1_raw0_1")
+        nc.vector.tensor_copy(x_last[:], x_window[1][:].bitcast(U32).indirect(offs_t[:, (S - LAST) // STRIPE :]))
 
-        def project(t, pieces, banks):
-            h = keep.tile([P, S], F32, name="h", tag="w1_block1" if t == 0 else "h%d" % t)
-            for (a, b), n in zip(pieces, banks):
-                acc = bank(n, "acc")
-                for z in range(PASSES):
-                    codes, plane = w1_mx[t, z]
+        def picked_words(z, a, b):
+            return x_last[:] if (z, a) == (1, S - LAST) else x_codes[z][:, a:b]
+
+        def project(t, width, banks):
+            h = sbuf([P, S], F32, "h%d" % t)
+            accs = [bank(n, "acc") for n in banks]
+            for z in range(PASSES):
+                codes, plane = w1_mx[t, z]
+                for a in range(0, S, LAST):
                     nc.tensor.matmul_mx(
-                        out=acc[:, 0 : b - a],
+                        out=accs[a // width][:, a % width : a % width + LAST],
                         lhsT=codes.bitcast(FP8X4),
                         lhsT_scale=plane,
-                        rhs=x_codes[z][:, a:b].bitcast(FP8X4),
-                        rhs_scale=x_plane[PACK * z : P, a:b],
-                        start=(z == 0),
-                        stop=(z == PASSES - 1),
+                        rhs=picked_words(z, a, a + LAST).bitcast(FP8X4),
+                        rhs_scale=x_plane[PACK * z : P, a : a + LAST],
+                        start=(z == 0 and a % width == 0),
+                        stop=(z == PASSES - 1 and (a + LAST) % width == 0),
                     )
-                nc.scalar.activation(out=h[:, a:b], in_=acc[:, 0 : b - a], func=ACT.Silu)
+            for i, acc in enumerate(accs):
+                nc.scalar.activation(out=h[:, i * width : (i + 1) * width], in_=acc[:, 0:width], func=ACT.Silu)
             return h
 
-        quantize_w1_block(1)
-        h_tiles = [project(0, first_pieces, (0, 1, 2))]
-        signed_gates = [gates[0]]
-        for d in range(1, D):
-            tile = keep.tile([P, V], F32, name="minus_gate%d" % d)
-            nc.scalar.mul(out=tile[:], in_=gates[d][:], mul=-1.0)
-            signed_gates.append(tile)
+        h_tiles = [project(0, 256, (3, 4, 5, 6))]
+        quantize_w1(1, [0], None)
+        quantize_w1(1, [1], "w1_codes0_1")
+        h_tiles.append(project(1, BANK, (7, 0)))
+        quantize_w1(2, [0, 1], "w1_codes0_1")
+        quantize_w1(3, [0, 1], "w1_codes1_1")
+        h_tiles.append(project(2, BANK, (1, 2)))
+        h_tiles.append(project(3, BANK, (3, 4)))
 
-        z_bf = [keep.tile([P, 2, P, 2], BF16, name="z_bf", tag="w1_block3" if vb == 0 else "z_bf%d" % vb) for vb in range(V_BLOCKS)]
-        slot_of = {(0, 0, 0): "staging1", (1, 0, 0): "staging2", (1, 1, 0): "staging3"}
+        z_bf = sbuf([P, V_BLOCKS, 2, P, 2], BF16, "z_bf", "w1_codes1_1")
 
-        def fetch_terms(t, a, b, each):
+        reuse = {(0, 1, 0): "w1_raw1_1"}
+        for n in range(D):
+            reuse[2, n, 3 * P] = "term3_%d_0" % (n + 1)
+            reuse[3, n, 3 * P] = "term3_%d_256" % (n + 1)
+
+        def laplacian(t, blocks, sum_bank):
+            a, b = blocks[0] * P, (blocks[-1] + 1) * P
             cols = slice(a // STRIPE, b // STRIPE)
-            first = None
+            terms = []
             for n in range(D + 1):
-                tag = slot_of.get((t, n, a), "term%d_%d_%d" % (t, n, a))
-                term = keep.tile([P, b - a], F32, name="term", tag=tag, align_bytes=64)
+                term = sbuf([P, b - a], F32, "term%d_%d_%d" % (t, n, a), reuse.get((t, n, a)))
                 if n < D:
                     nc.vector.tensor_tensor(
                         term[:], h_tiles[t][:].indirect(pos_t[n][:, cols]), signed_gates[n][:, a:b], MULT
                     )
                 else:
-                    nc.vector.tensor_tensor(term[:], h_tiles[t][:].indirect(cen_t[:, cols]), first[:], SUBTRACT)
-                if n == 0:
-                    first = term
-                else:
-                    each(n, term)
-
-        def add_turned(dst, src, n):
-            nc.tensor.matmul(dst, lhsT=src, rhs=ident[:], is_transpose=True, start=(n == 1), stop=(n == D))
-
-        def round_block(t, vb, src):
-            nc.scalar.copy(
-                out=z_bf[vb][:, :, QUAD * t : QUAD * (t + 1), :],
-                in_=src.rearrange("v (m u e) -> v u m e", u=2, e=2),
-            )
-
-        def sum_late(t, n_bank):
-            terms = {}
-            fetch_terms(t, 0, V, terms.setdefault)
-            total = bank(n_bank, "z_sum")
-            for vb in range(V_BLOCKS):
+                    nc.vector.tensor_tensor(term[:], h_tiles[t][:].indirect(cen_t[:, cols]), terms[0][:], SUBTRACT)
+                terms.append(term)
+            total = bank(sum_bank, "z_sum")
+            for i in range(len(blocks)):
                 for n in range(1, D + 1):
-                    add_turned(total[:, vb * P : (vb + 1) * P], terms[n][:, vb * P : (vb + 1) * P], n)
-            for vb in range(V_BLOCKS):
-                round_block(t, vb, total[:, vb * P : (vb + 1) * P])
-
-        def sum_at_once(t, blocks, bank_numbers):
-            a = blocks[0] * P
-            banks = {vb: bank(n, "z_sum") for vb, n in zip(blocks, bank_numbers)}
-
-            def each(n, term):
-                for vb in blocks:
-                    add_turned(banks[vb][:, 0:P], term[:, vb * P - a : (vb + 1) * P - a], n)
-
-            fetch_terms(t, a, (blocks[-1] + 1) * P, each)
-            for vb in blocks:
-                round_block(t, vb, banks[vb][:, 0:P])
+                    nc.tensor.matmul(
+                        total[:, i * P : (i + 1) * P],
+                        lhsT=terms[n][:, i * P : (i + 1) * P],
+                        rhs=ident[:],
+                        is_transpose=True,
+                        start=(n == 1),
+                        stop=(n == D),
+                    )
+            nc.scalar.copy(
+                out=z_bf[:, blocks[0] : blocks[-1] + 1, :, QUAD * t : QUAD * (t + 1), :],
+                in_=total[:, 0 : b - a].rearrange("v (i m u e) -> v i u m e", m=QUAD, u=2, e=2),
+            )
 
         def turn_back(blocks, turn_bank):
             first, width = blocks[0], len(blocks) * P
             turned = bank(turn_bank, "turned")
             for i, vb in enumerate(blocks):
-                words = z_bf[vb][:].rearrange("v u m e -> v (u m e)").bitcast(F32)
+                words = z_bf[:, vb].rearrange("v u m e -> v (u m e)").bitcast(F32)
                 for u in range(2):
                     at = u * width + i * P
                     nc.tensor.transpose(turned[:, at : at + P], words[:, u * P : (u + 1) * P], ident[:])
-            grouped = keep.tile([P, width, 2], F32, name="z_grouped", tag="z_words%d" % first, align_bytes=64)
+            grouped = sbuf([P, width, 2], F32, "z_grouped%d" % first)
             nc.scalar.copy(out=grouped[:], in_=turned[:, 0 : 2 * width].rearrange("m (u v) -> m v u", u=2))
-            codes = keep.tile([P, width], U32, name="z_codes%d" % first, align_bytes=64)
-            plane = keep.tile([P, width], U8, name="z_plane%d" % first, align_bytes=64)
+            return first, width, grouped
+
+        def quantize_z(first, width, grouped, codes_tag):
+            codes = sbuf([P, width], U32, "z_codes%d" % first, codes_tag)
+            plane = sbuf([P, width], U8, "z_plane%d" % first)
             nc.vector.quantize_mx(
                 out=codes[:].bitcast(FP8X4),
                 scales=plane[:],
@@ -244,7 +244,7 @@ def tile_picked_lapl_silu_p_kernel(
             )
             return first * P, codes, plane
 
-        def project_out(groups, leave, out_bank):
+        def project_out(groups, out_bank):
             first = groups[0][0]
             acc = bank(out_bank, "out_acc")
             for start, codes, plane in groups:
@@ -258,24 +258,19 @@ def tile_picked_lapl_silu_p_kernel(
                     start=True,
                     stop=True,
                 )
-            result = keep.tile([P, end], F32, name="result%d" % first)
-            leave(out=result[:], in_=acc[:, 0:end])
+            result = sbuf([P, end], F32, "result%d" % first)
+            nc.vector.tensor_copy(out=result[:], in_=acc[:, 0:end])
             nc.sync.dma_start(out=out[:, first : first + end], in_=result[:])
 
-        halves = [(0, BANK), (BANK, S)]
-        h_tiles.append(project(1, halves, (3, 4)))
-        for t, banks in ((2, (1, 2)), (3, (3, 4))):
-            quantize_w1_block(t)
-            h_tiles.append(project(t, halves, banks))
-        sum_at_once(0, [0, 1, 2, 3], [5, 6, 7, 0])
-        sum_late(1, 4)
-        sum_at_once(2, [0, 1, 2], [0, 1, 2])
-        sum_at_once(3, [0, 1], [3, 5])
-        early = [turn_back([0, 1], 6)]
-        sum_at_once(3, [2], [5])
-        sum_at_once(2, [3], [6])
-        early.append(turn_back([2], 7))
-        sum_at_once(3, [3], [7])
-        last = turn_back([3], 0)
-        project_out(early, nc.scalar.copy, 7)
-        project_out([last], nc.vector.tensor_copy, 2)
+        laplacian(0, [0, 1, 2, 3], 0)
+        laplacian(1, [0, 1, 2, 3], 4)
+        laplacian(2, [0, 1, 2], 3)
+        laplacian(3, [0, 1], 5)
+        turned = [turn_back([0, 1], 1)]
+        laplacian(3, [2], 6)
+        turned.append(turn_back([2], 2))
+        laplacian(2, [3], 1)
+        laplacian(3, [3], 2)
+        turned.append(turn_back([3], 3))
+        project_out([quantize_z(*turned[0], "term3_1_256"), quantize_z(*turned[1], None)], 2)
+        project_out([quantize_z(*turned[2], None)], 5)

@@ -28,6 +28,12 @@ QUADS = 4
 QUAD = 32
 LAST = 256
 PLACES = {
+    "picked_scales": 0,
+    "w1_raw1_0": 11264,
+    "w1_raw1_1": 13312,
+    "term0_1_0": 13312,
+    "w2_codes": 15360,
+    "w2_plane": 15872,
     "term1_0_0": 0,
     "w1_raw2": 1024,
     "term1_1_0": 2048,
@@ -74,28 +80,43 @@ def tile_picked_lapl_silu_p_kernel(
             return tile
 
         scale_window = sbuf([P, T], U8, "scale_window")
-        nc.gpsimd.memset(scale_window[:].bitcast(I32), 0)
+        nc.vector.memset(scale_window[QUAD : 2 * QUAD, :].bitcast(I32), 0)
+        nc.vector.memset(scale_window[2 * QUAD : P, :].bitcast(I32), 0)
+        x_plane = sbuf([P, S], U8, "x_plane")
+        nc.vector.memset(x_plane[:].bitcast(I32), 0)
+        gate_row = sbuf([P, D, PACK], F32, "gate_row")
+        nc.scalar.dma_start(out=gate_row[:], in_=gate[:, 0, :].rearrange("d (p j) -> p d j", j=PACK))
         warm = sbuf([P, 2], F32, "warm")
         nc.vector.memset(warm[:, 0:1], 0.0)
         nc.scalar.activation(out=warm[:, 1:2], in_=warm[:, 0:1], func=ACT.Silu)
 
-        offs_t = load_list(offs, "offs_t")
-        gate_row = sbuf([P, D, PACK], F32, "gate_row")
-        nc.sync.dma_start(out=gate_row[:], in_=gate[:, 0, :].rearrange("d (p j) -> p d j", j=PACK))
-        for q in range(QUADS):
-            nc.sync.dma_start(
-                out=scale_window[QUAD * q : QUAD * q + PASSES * PACK, :].bitcast(I32),
-                in_=x_scales[:, PACK * q : PACK * (q + 1), :].bitcast(I32),
-            )
-        x_window = []
-        w1_raw = {}
         for z in range(PASSES):
-            x_window.append(load_words(z))
-            w1_raw[0, z] = load_w1(0, [z])
+            nc.sync.dma_start(
+                out=scale_window[STRIPE * z : STRIPE * (z + 1), :].bitcast(I32),
+                in_=x_scales[z].rearrange("(q r) n -> r q n", r=PACK).bitcast(I32),
+            )
+        offs_t = load_list(offs, "offs_t")
+        x_window = [load_words(0)]
+        pos_t = [load_list(pos1, "pos_t0"), load_list(pos2, "pos_t1")]
+        w1_raw = {(0, 0): load_w1(0, [0])}
+        x_window.append(load_words(1))
+        w1_raw[0, 1] = load_w1(0, [1])
+        pos_t.append(load_list(pos3, "pos_t2"))
+        cen_t = load_list(cen, "cen_t")
+
+        def pick(dst, window, a, b):
+            nc.vector.tensor_copy(dst[:, a:b], window.indirect(offs_t[:, a // STRIPE : b // STRIPE]))
+
+        picked_scales = sbuf([P, 16 * S], U8, "picked_scales")
+        pick(picked_scales, scale_window[:], 0, S)
+        for q in range(QUADS):
+            nc.scalar.dma_start(
+                out=x_plane[QUAD * q : QUAD * q + PASSES * PACK, :].bitcast(I32),
+                in_=picked_scales[q:QUAD:QUADS, 0:S].bitcast(I32),
+            )
+
         for z in range(PASSES):
             w1_raw[1, z] = load_w1(1, [z])
-        pos_t = [load_list(source, "pos_t%d" % d) for d, source in enumerate((pos1, pos2, pos3))]
-        cen_t = load_list(cen, "cen_t")
         for t in range(2, H_TILES):
             w1_raw[t, 0] = load_w1(t, [0, 1])
         w2_codes = sbuf([P, N], I32, "w2_codes")
@@ -140,13 +161,8 @@ def tile_picked_lapl_silu_p_kernel(
             for i, z in enumerate(passes):
                 w1_mx[t, z] = (codes[:, i * P : (i + 1) * P], plane[:, i * P : (i + 1) * P])
 
-        x_plane = sbuf([P, S], U8, "x_plane")
         x_codes = [sbuf([P, S], U32, "x_codes0"), sbuf([P, S - LAST], U32, "x_codes1")]
 
-        def pick(dst, window, a, b):
-            nc.vector.tensor_copy(dst[:, a:b], window.indirect(offs_t[:, a // STRIPE : b // STRIPE]))
-
-        pick(x_plane, scale_window[:], 0, S)
         pick(x_codes[0], x_window[0][:].bitcast(U32), 0, S)
         quantize_w1(0, [0], None)
         for a, b in [(0, 512), (512, S - LAST)]:
@@ -188,7 +204,7 @@ def tile_picked_lapl_silu_p_kernel(
 
         z_bf = sbuf([P, V_BLOCKS, 2, P, 2], BF16, "z_bf", "w1_codes1_1")
 
-        reuse = {(0, 1, 0): "w1_raw1_1"}
+        reuse = {}
         for n in range(D):
             reuse[2, n, 3 * P] = "term3_%d_0" % (n + 1)
             reuse[3, n, 3 * P] = "term3_%d_256" % (n + 1)
@@ -207,15 +223,15 @@ def tile_picked_lapl_silu_p_kernel(
                     nc.vector.tensor_tensor(term[:], h_tiles[t][:].indirect(cen_t[:, cols]), terms[0][:], SUBTRACT)
                 terms.append(term)
             total = bank(sum_bank, "z_sum")
-            for i in range(len(blocks)):
-                for n in range(1, D + 1):
+            for n in range(1, D + 1):
+                for i in range(len(blocks)):
                     nc.tensor.matmul(
                         total[:, i * P : (i + 1) * P],
                         lhsT=terms[n][:, i * P : (i + 1) * P],
                         rhs=ident[:],
                         is_transpose=True,
-                        start=(n == 1),
-                        stop=(n == D),
+                        start=(n == 1 and i == 0),
+                        stop=(n == D and i == len(blocks) - 1),
                     )
             nc.scalar.copy(
                 out=z_bf[:, blocks[0] : blocks[-1] + 1, :, QUAD * t : QUAD * (t + 1), :],
@@ -244,7 +260,7 @@ def tile_picked_lapl_silu_p_kernel(
             )
             return first * P, codes, plane
 
-        def project_out(groups, out_bank):
+        def project_out(groups, out_bank, leave):
             first = groups[0][0]
             acc = bank(out_bank, "out_acc")
             for start, codes, plane in groups:
@@ -259,7 +275,7 @@ def tile_picked_lapl_silu_p_kernel(
                     stop=True,
                 )
             result = sbuf([P, end], F32, "result%d" % first)
-            nc.vector.tensor_copy(out=result[:], in_=acc[:, 0:end])
+            leave(out=result[:], in_=acc[:, 0:end])
             nc.sync.dma_start(out=out[:, first : first + end], in_=result[:])
 
         laplacian(0, [0, 1, 2, 3], 0)
@@ -272,5 +288,5 @@ def tile_picked_lapl_silu_p_kernel(
         laplacian(2, [3], 1)
         laplacian(3, [3], 2)
         turned.append(turn_back([3], 3))
-        project_out([quantize_z(*turned[0], "term3_1_256"), quantize_z(*turned[1], None)], 2)
-        project_out([quantize_z(*turned[2], None)], 5)
+        project_out([quantize_z(*turned[0], "term3_1_256"), quantize_z(*turned[1], None)], 2, nc.scalar.copy)
+        project_out([quantize_z(*turned[2], None)], 5, nc.vector.tensor_copy)

@@ -28,19 +28,27 @@ QUADS = 4
 QUAD = 32
 LAST = 256
 PLACES = {
-    "picked_scales": 0,
-    "w1_raw1_0": 11264,
-    "w1_raw1_1": 13312,
-    "term0_1_0": 13312,
-    "w2_codes": 15360,
-    "w2_plane": 15872,
+    "w1_raw0_0": 0,
+    "scale_window": 32768,
+    "w1_bf0_0": 32768,
     "term1_0_0": 0,
     "w1_raw2": 1024,
     "term1_1_0": 2048,
     "term1_2_0": 5120,
     "w1_raw3": 6144,
     "h2": 7168,
+    "w1_raw1_0": 13312,
+    "term0_0_0": 15360,
+    "w1_raw1_1": 16384,
+    "term0_1_0": 17408,
+    "term0_2_0": 19456,
+    "w2_codes": 21504,
+    "w2_plane": 22016,
+    "x_window1": 24576,
+    "w1_bf1_0": 24576,
+    "w1_bf1_1": 25600,
 }
+SPANS = {"w1_raw0_0": 11, "w1_raw1_1": 2}
 
 
 def tile_picked_lapl_silu_p_kernel(
@@ -73,11 +81,11 @@ def tile_picked_lapl_silu_p_kernel(
 
         def load_w1(t, passes):
             name = "w1_raw%d" % t if len(passes) == PASSES else "w1_raw%d_%d" % (t, passes[0])
-            tile = sbuf([P, len(passes), PACK, P], F32, name)
+            tile = sbuf([P, SPANS.get(name, len(passes)), PACK, P], F32, name)
             for i, z in enumerate(passes):
                 rows = w1[z * P * PACK : (z + 1) * P * PACK, t * P : (t + 1) * P]
                 nc.sync.dma_start(out=tile[:, i], in_=rows.rearrange("(p j) c -> p j c", j=PACK))
-            return tile
+            return tile[:, 0 : len(passes)]
 
         scale_window = sbuf([P, T], U8, "scale_window")
         nc.vector.memset(scale_window[QUAD : 2 * QUAD, :].bitcast(I32), 0)
@@ -107,26 +115,12 @@ def tile_picked_lapl_silu_p_kernel(
         def pick(dst, window, a, b):
             nc.vector.tensor_copy(dst[:, a:b], window.indirect(offs_t[:, a // STRIPE : b // STRIPE]))
 
-        picked_scales = sbuf([P, 16 * S], U8, "picked_scales")
+        picked_scales = sbuf([P, S], U8, "picked_scales")
         pick(picked_scales, scale_window[:], 0, S)
         for q in range(QUADS):
             nc.scalar.dma_start(
                 out=x_plane[QUAD * q : QUAD * q + PASSES * PACK, :].bitcast(I32),
                 in_=picked_scales[q:QUAD:QUADS, 0:S].bitcast(I32),
-            )
-
-        for z in range(PASSES):
-            w1_raw[1, z] = load_w1(1, [z])
-        for t in range(2, H_TILES):
-            w1_raw[t, 0] = load_w1(t, [0, 1])
-        w2_codes = sbuf([P, N], I32, "w2_codes")
-        nc.sync.dma_start(out=w2_codes[:], in_=w2_words[0].rearrange("p n j -> p (n j)").bitcast(I32))
-        w2_plane = sbuf([P, N], U8, "w2_plane")
-        nc.gpsimd.memset(w2_plane[:].bitcast(I32), 0)
-        for q in range(QUADS):
-            nc.sync.dma_start(
-                out=w2_plane[QUAD * q : QUAD * q + PACK, :].bitcast(I32),
-                in_=w2_scales[0, PACK * q : PACK * (q + 1), :].bitcast(I32),
             )
 
         ident = sbuf([P, P], F32, "ident")
@@ -145,14 +139,19 @@ def tile_picked_lapl_silu_p_kernel(
 
         w1_mx = {}
 
-        def quantize_w1(t, passes, staging_tag):
+        def cast_w1(t, passes, staging_tag, cast):
             n = len(passes)
             name = "%d_%d" % (t, passes[0])
             grouped = sbuf([P, n, P, PACK], BF16, "w1_bf" + name, staging_tag)
-            nc.scalar.copy(
+            cast(
                 out=grouped[:].rearrange("p z (c i) j -> p z c j i", i=PACK),
-                in_=w1_raw[t, passes[0]][:].rearrange("p z j (c i) -> p z c j i", i=PACK),
+                in_=w1_raw[t, passes[0]].rearrange("p z j (c i) -> p z c j i", i=PACK),
             )
+            return t, passes, grouped
+
+        def quantize_w1(t, passes, grouped):
+            n = len(passes)
+            name = "%d_%d" % (t, passes[0])
             codes = sbuf([P, n * P], U32, "w1_codes" + name)
             plane = sbuf([P, n * P], U8, "w1_plane" + name)
             nc.vector.quantize_mx(
@@ -164,10 +163,24 @@ def tile_picked_lapl_silu_p_kernel(
         x_codes = [sbuf([P, S], U32, "x_codes0"), sbuf([P, S - LAST], U32, "x_codes1")]
 
         pick(x_codes[0], x_window[0][:].bitcast(U32), 0, S)
-        quantize_w1(0, [0], None)
+        quantize_w1(*cast_w1(0, [0], None, nc.scalar.copy))
+        for z in range(PASSES):
+            w1_raw[1, z] = load_w1(1, [z])
+        for t in range(2, H_TILES):
+            w1_raw[t, 0] = load_w1(t, [0, 1])
+        w2_codes = sbuf([P, N], I32, "w2_codes")
+        nc.sync.dma_start(out=w2_codes[:], in_=w2_words[0].rearrange("p n j -> p (n j)").bitcast(I32))
+        w2_plane = sbuf([P, N], U8, "w2_plane")
+        nc.gpsimd.memset(w2_plane[:].bitcast(I32), 0)
+        for q in range(QUADS):
+            nc.sync.dma_start(
+                out=w2_plane[QUAD * q : QUAD * q + PACK, :].bitcast(I32),
+                in_=w2_scales[0, PACK * q : PACK * (q + 1), :].bitcast(I32),
+            )
+
         for a, b in [(0, 512), (512, S - LAST)]:
             pick(x_codes[1], x_window[1][:].bitcast(U32), a, b)
-        quantize_w1(0, [1], None)
+        quantize_w1(*cast_w1(0, [1], None, nc.scalar.copy))
         x_last = sbuf([P, LAST], U32, "x_last", "w1_raw0_1")
         nc.vector.tensor_copy(x_last[:], x_window[1][:].bitcast(U32).indirect(offs_t[:, (S - LAST) // STRIPE :]))
 
@@ -194,11 +207,11 @@ def tile_picked_lapl_silu_p_kernel(
             return h
 
         h_tiles = [project(0, 256, (3, 4, 5, 6))]
-        quantize_w1(1, [0], None)
-        quantize_w1(1, [1], "w1_codes0_1")
+        for staged in [cast_w1(1, [z], None, nc.vector.tensor_copy) for z in range(PASSES)]:
+            quantize_w1(*staged)
         h_tiles.append(project(1, BANK, (7, 0)))
-        quantize_w1(2, [0, 1], "w1_codes0_1")
-        quantize_w1(3, [0, 1], "w1_codes1_1")
+        quantize_w1(*cast_w1(2, [0, 1], "w1_codes0_1", nc.scalar.copy))
+        quantize_w1(*cast_w1(3, [0, 1], "w1_codes1_1", nc.scalar.copy))
         h_tiles.append(project(2, BANK, (1, 2)))
         h_tiles.append(project(3, BANK, (3, 4)))
 

@@ -28,9 +28,6 @@ QUADS = 4
 QUAD = 32
 LAST = 256
 PLACES = {
-    "w1_raw0_0": 0,
-    "scale_window": 32768,
-    "w1_bf0_0": 32768,
     "term1_0_0": 0,
     "w1_raw2": 1024,
     "term1_1_0": 2048,
@@ -38,17 +35,13 @@ PLACES = {
     "w1_raw3": 6144,
     "h2": 7168,
     "w1_raw1_0": 13312,
-    "term0_0_0": 15360,
+    "term0_0_0": 13312,
+    "term0_1_0": 15360,
     "w1_raw1_1": 16384,
-    "term0_1_0": 17408,
-    "term0_2_0": 19456,
-    "w2_codes": 21504,
-    "w2_plane": 22016,
+    "term0_2_0": 17408,
     "x_window1": 24576,
     "w1_bf1_0": 24576,
-    "w1_bf1_1": 25600,
 }
-SPANS = {"w1_raw0_0": 11, "w1_raw1_1": 2}
 
 
 def tile_picked_lapl_silu_p_kernel(
@@ -81,11 +74,11 @@ def tile_picked_lapl_silu_p_kernel(
 
         def load_w1(t, passes):
             name = "w1_raw%d" % t if len(passes) == PASSES else "w1_raw%d_%d" % (t, passes[0])
-            tile = sbuf([P, SPANS.get(name, len(passes)), PACK, P], F32, name)
+            tile = sbuf([P, len(passes), PACK, P], F32, name)
             for i, z in enumerate(passes):
                 rows = w1[z * P * PACK : (z + 1) * P * PACK, t * P : (t + 1) * P]
                 nc.sync.dma_start(out=tile[:, i], in_=rows.rearrange("(p j) c -> p j c", j=PACK))
-            return tile[:, 0 : len(passes)]
+            return tile[:]
 
         scale_window = sbuf([P, T], U8, "scale_window")
         nc.vector.memset(scale_window[QUAD : 2 * QUAD, :].bitcast(I32), 0)
@@ -105,12 +98,9 @@ def tile_picked_lapl_silu_p_kernel(
             )
         offs_t = load_list(offs, "offs_t")
         x_window = [load_words(0)]
-        pos_t = [load_list(pos1, "pos_t0"), load_list(pos2, "pos_t1")]
         w1_raw = {(0, 0): load_w1(0, [0])}
         x_window.append(load_words(1))
         w1_raw[0, 1] = load_w1(0, [1])
-        pos_t.append(load_list(pos3, "pos_t2"))
-        cen_t = load_list(cen, "cen_t")
 
         def pick(dst, window, a, b):
             nc.vector.tensor_copy(dst[:, a:b], window.indirect(offs_t[:, a // STRIPE : b // STRIPE]))
@@ -118,10 +108,27 @@ def tile_picked_lapl_silu_p_kernel(
         picked_scales = sbuf([P, S], U8, "picked_scales")
         pick(picked_scales, scale_window[:], 0, S)
         for q in range(QUADS):
-            nc.scalar.dma_start(
+            nc.sync.dma_start(
                 out=x_plane[QUAD * q : QUAD * q + PASSES * PACK, :].bitcast(I32),
                 in_=picked_scales[q:QUAD:QUADS, 0:S].bitcast(I32),
             )
+
+        for z in range(PASSES):
+            w1_raw[1, z] = load_w1(1, [z])
+        pos_t = [load_list(source, "pos_t%d" % d) for d, source in enumerate((pos1, pos2, pos3))]
+        cen_t = load_list(cen, "cen_t")
+        for t in range(2, H_TILES):
+            w1_raw[t, 0] = load_w1(t, [0, 1])
+        w2_codes = sbuf([P, N], I32, "w2_codes")
+        nc.sync.dma_start(out=w2_codes[:], in_=w2_words[0].rearrange("p n j -> p (n j)").bitcast(I32))
+        w2_plane = sbuf([P, N], U8, "w2_plane")
+        nc.gpsimd.memset(w2_plane[:].bitcast(I32), 0)
+        for q in range(QUADS):
+            nc.sync.dma_start(
+                out=w2_plane[QUAD * q : QUAD * q + PACK, :].bitcast(I32),
+                in_=w2_scales[0, PACK * q : PACK * (q + 1), :].bitcast(I32),
+            )
+
 
         ident = sbuf([P, P], F32, "ident")
         make_identity(nc, ident[:])
@@ -164,20 +171,6 @@ def tile_picked_lapl_silu_p_kernel(
 
         pick(x_codes[0], x_window[0][:].bitcast(U32), 0, S)
         quantize_w1(*cast_w1(0, [0], None, nc.scalar.copy))
-        for z in range(PASSES):
-            w1_raw[1, z] = load_w1(1, [z])
-        for t in range(2, H_TILES):
-            w1_raw[t, 0] = load_w1(t, [0, 1])
-        w2_codes = sbuf([P, N], I32, "w2_codes")
-        nc.sync.dma_start(out=w2_codes[:], in_=w2_words[0].rearrange("p n j -> p (n j)").bitcast(I32))
-        w2_plane = sbuf([P, N], U8, "w2_plane")
-        nc.gpsimd.memset(w2_plane[:].bitcast(I32), 0)
-        for q in range(QUADS):
-            nc.sync.dma_start(
-                out=w2_plane[QUAD * q : QUAD * q + PACK, :].bitcast(I32),
-                in_=w2_scales[0, PACK * q : PACK * (q + 1), :].bitcast(I32),
-            )
-
         for a, b in [(0, 512), (512, S - LAST)]:
             pick(x_codes[1], x_window[1][:].bitcast(U32), a, b)
         quantize_w1(*cast_w1(0, [1], None, nc.scalar.copy))
@@ -207,8 +200,8 @@ def tile_picked_lapl_silu_p_kernel(
             return h
 
         h_tiles = [project(0, 256, (3, 4, 5, 6))]
-        for staged in [cast_w1(1, [z], None, nc.vector.tensor_copy) for z in range(PASSES)]:
-            quantize_w1(*staged)
+        quantize_w1(*cast_w1(1, [0], None, nc.vector.tensor_copy))
+        quantize_w1(*cast_w1(1, [1], "w1_codes0_1", nc.scalar.copy))
         h_tiles.append(project(1, BANK, (7, 0)))
         quantize_w1(*cast_w1(2, [0, 1], "w1_codes0_1", nc.scalar.copy))
         quantize_w1(*cast_w1(3, [0, 1], "w1_codes1_1", nc.scalar.copy))

@@ -85,8 +85,8 @@ def tile_picked_lapl_silu_p_kernel(
         nc.vector.memset(scale_window[2 * QUAD : P, :].bitcast(I32), 0)
         x_plane = sbuf([P, S], U8, "x_plane")
         nc.vector.memset(x_plane[:].bitcast(I32), 0)
-        gate_row = sbuf([P, D, PACK], F32, "gate_row")
-        nc.scalar.dma_start(out=gate_row[:], in_=gate[:, 0, :].rearrange("d (p j) -> p d j", j=PACK))
+        gate_rows = sbuf([P, D, P], F32, "gate_rows")
+        nc.gpsimd.memset(gate_rows[:], 0.0)
         warm = sbuf([P, 2], F32, "warm")
         nc.vector.memset(warm[:, 0:1], 0.0)
         nc.scalar.activation(out=warm[:, 1:2], in_=warm[:, 0:1], func=ACT.Silu)
@@ -97,6 +97,7 @@ def tile_picked_lapl_silu_p_kernel(
                 in_=x_scales[z].rearrange("(q r) n -> r q n", r=PACK).bitcast(I32),
             )
         offs_t = load_list(offs, "offs_t")
+        nc.sync.dma_start(out=gate_rows[0:V_BLOCKS], in_=gate[:, 0, :].rearrange("d (c n) -> c d n", n=P))
         x_window = [load_words(0)]
         w1_raw = {(0, 0): load_w1(0, [0])}
         x_window.append(load_words(1))
@@ -133,16 +134,23 @@ def tile_picked_lapl_silu_p_kernel(
         ident = sbuf([P, P], F32, "ident")
         make_identity(nc, ident[:])
 
+        upright = bank(7, "gate_upright")
+        for d in range(D):
+            nc.tensor.transpose(upright[:, d * P : (d + 1) * P], gate_rows[:, d, :], ident[:])
+        gate_columns = sbuf([P, D, V_BLOCKS], F32, "gate_columns")
+        nc.scalar.copy(
+            out=gate_columns[:], in_=upright[:, 0 : D * P].rearrange("n (d c) -> n d c", d=D)[:, :, 0:V_BLOCKS]
+        )
         signed_gates = []
         for d in range(D):
             spread = bank(d, "gate_spread")
-            for j in range(PACK):
+            for c in range(V_BLOCKS):
                 nc.tensor.transpose(
-                    spread[:, j * P : (j + 1) * P], gate_row[:, d, j : j + 1].to_broadcast([P, P]), ident[:]
+                    spread[:, c * P : (c + 1) * P], gate_columns[:, d, c : c + 1].to_broadcast([P, P]), ident[:]
                 )
-            tile = sbuf([P, P, PACK], F32, "signed_gate%d" % d)
-            nc.scalar.mul(out=tile[:], in_=spread[:].rearrange("p (j n) -> p n j", j=PACK), mul=1.0 if d == 0 else -1.0)
-            signed_gates.append(tile[:].rearrange("p n j -> p (n j)"))
+            tile = sbuf([P, V], F32, "signed_gate%d" % d)
+            nc.scalar.mul(out=tile[:], in_=spread[:], mul=1.0 if d == 0 else -1.0)
+            signed_gates.append(tile)
 
         w1_mx = {}
 

@@ -27,18 +27,16 @@ STRIPE = 16
 QUADS = 4
 QUAD = 32
 LAST = 256
+HALF = 64
 PLACES = {
-    "term1_0_0": 0,
-    "w1_raw2": 1024,
-    "term1_1_0": 2048,
-    "term1_2_0": 5120,
-    "w1_raw3": 6144,
-    "h2": 7168,
+    "w1_upper1": 0,
+    "h1": 0,
     "w1_raw1_0": 13312,
     "term0_0_0": 13312,
     "term0_1_0": 15360,
     "w1_raw1_1": 16384,
     "term0_2_0": 17408,
+    "w1_bf_upper": 19456,
     "x_window1": 24576,
     "w1_bf1_0": 24576,
 }
@@ -72,13 +70,11 @@ def tile_picked_lapl_silu_p_kernel(
             nc.sync.dma_start(out=tile[:], in_=x_words[z].rearrange("p n j -> p (n j)").bitcast(I32))
             return tile
 
-        def load_w1(t, passes):
-            name = "w1_raw%d" % t if len(passes) == PASSES else "w1_raw%d_%d" % (t, passes[0])
-            tile = sbuf([P, len(passes), PACK, P], F32, name)
-            for i, z in enumerate(passes):
-                rows = w1[z * P * PACK : (z + 1) * P * PACK, t * P : (t + 1) * P]
-                nc.sync.dma_start(out=tile[:, i], in_=rows.rearrange("(p j) c -> p j c", j=PACK))
-            return tile[:]
+        def load_w1(name, z, first, width, span=1):
+            tile = sbuf([P, span, PACK, width], F32, name)
+            rows = w1[z * P * PACK : (z + 1) * P * PACK, first : first + width]
+            nc.sync.dma_start(out=tile[:, 0], in_=rows.rearrange("(p j) c -> p j c", j=PACK))
+            return tile[:, 0]
 
         scale_window = sbuf([P, T], U8, "scale_window")
         nc.vector.memset(scale_window[QUAD : 2 * QUAD, :].bitcast(I32), 0)
@@ -99,9 +95,9 @@ def tile_picked_lapl_silu_p_kernel(
         offs_t = load_list(offs, "offs_t")
         nc.sync.dma_start(out=gate_rows[0:V_BLOCKS], in_=gate[:, 0, :].rearrange("d (c n) -> c d n", n=P))
         x_window = [load_words(0)]
-        w1_raw = {(0, 0): load_w1(0, [0])}
+        w1_raw = {(0, 0): load_w1("w1_raw0_0", 0, 0, P)}
         x_window.append(load_words(1))
-        w1_raw[0, 1] = load_w1(0, [1])
+        w1_raw[0, 1] = load_w1("w1_raw0_1", 1, 0, P)
 
         def pick(dst, window, a, b):
             nc.vector.tensor_copy(dst[:, a:b], window.indirect(offs_t[:, a // STRIPE : b // STRIPE]))
@@ -115,11 +111,10 @@ def tile_picked_lapl_silu_p_kernel(
             )
 
         for z in range(PASSES):
-            w1_raw[1, z] = load_w1(1, [z])
+            w1_raw[1, z] = load_w1("w1_raw1_%d" % z, z, P, P, 1 + z)
         pos_t = [load_list(source, "pos_t%d" % d) for d, source in enumerate((pos1, pos2, pos3))]
         cen_t = load_list(cen, "cen_t")
-        for t in range(2, H_TILES):
-            w1_raw[t, 0] = load_w1(t, [0, 1])
+        w1_upper = [load_w1("w1_upper%d" % z, z, 2 * P, 2 * P) for z in range(PASSES)]
         w2_codes = sbuf([P, N], I32, "w2_codes")
         nc.sync.dma_start(out=w2_codes[:], in_=w2_words[0].rearrange("p n j -> p (n j)").bitcast(I32))
         w2_plane = sbuf([P, N], U8, "w2_plane")
@@ -154,34 +149,41 @@ def tile_picked_lapl_silu_p_kernel(
 
         w1_mx = {}
 
-        def cast_w1(t, passes, staging_tag, cast):
-            n = len(passes)
-            name = "%d_%d" % (t, passes[0])
-            grouped = sbuf([P, n, P, PACK], BF16, "w1_bf" + name, staging_tag)
-            cast(
-                out=grouped[:].rearrange("p z (c i) j -> p z c j i", i=PACK),
-                in_=w1_raw[t, passes[0]].rearrange("p z j (c i) -> p z c j i", i=PACK),
-            )
-            return t, passes, grouped
+        def quantize(grouped, width, name, codes_tag=None):
+            codes = sbuf([P, width], U32, "codes_" + name, codes_tag)
+            plane = sbuf([P, width], U8, "plane_" + name)
+            nc.vector.quantize_mx(out=codes[:].bitcast(FP8X4), scales=plane[:], in_=grouped)
+            return codes, plane
 
-        def quantize_w1(t, passes, grouped):
-            n = len(passes)
-            name = "%d_%d" % (t, passes[0])
-            codes = sbuf([P, n * P], U32, "w1_codes" + name)
-            plane = sbuf([P, n * P], U8, "w1_plane" + name)
-            nc.vector.quantize_mx(
-                out=codes[:].bitcast(FP8X4), scales=plane[:], in_=grouped[:].rearrange("p z c j -> p (z c j)")
+        def quantize_w1(t, z, cast, staging_tag=None):
+            grouped = sbuf([P, P, PACK], BF16, "w1_bf%d_%d" % (t, z), staging_tag)
+            cast(
+                out=grouped[:].rearrange("p (c i) j -> p c j i", i=PACK),
+                in_=w1_raw[t, z].rearrange("p j (c i) -> p c j i", i=PACK),
             )
-            for i, z in enumerate(passes):
-                w1_mx[t, z] = (codes[:, i * P : (i + 1) * P], plane[:, i * P : (i + 1) * P])
+            codes, plane = quantize(grouped[:].rearrange("p c j -> p (c j)"), P, "w1_%d_%d" % (t, z))
+            w1_mx[t, z] = (codes[:], plane[:])
+
+        def quantize_w1_upper():
+            grouped = sbuf([P, 2, PASSES, HALF, 2, PACK], BF16, "w1_bf_upper")
+            for z in range(PASSES):
+                nc.scalar.copy(
+                    out=grouped[:, :, z].rearrange("p u m e j -> p u m j e"),
+                    in_=w1_upper[z].rearrange("p j (m u e) -> p u m j e", u=2, e=2),
+                )
+            codes, plane = quantize(grouped[:].rearrange("p u z m e j -> p (u z m e j)"), 2 * PASSES * P, "w1_upper")
+            for u in range(2):
+                for z in range(PASSES):
+                    at = (u * PASSES + z) * P
+                    w1_mx[2 + u, z] = (codes[:, at : at + P], plane[:, at : at + P])
 
         x_codes = [sbuf([P, S], U32, "x_codes0"), sbuf([P, S - LAST], U32, "x_codes1")]
 
         pick(x_codes[0], x_window[0][:].bitcast(U32), 0, S)
-        quantize_w1(*cast_w1(0, [0], None, nc.scalar.copy))
+        quantize_w1(0, 0, nc.scalar.copy)
         for a, b in [(0, 512), (512, S - LAST)]:
             pick(x_codes[1], x_window[1][:].bitcast(U32), a, b)
-        quantize_w1(*cast_w1(0, [1], None, nc.scalar.copy))
+        quantize_w1(0, 1, nc.scalar.copy)
         x_last = sbuf([P, LAST], U32, "x_last", "w1_raw0_1")
         nc.vector.tensor_copy(x_last[:], x_window[1][:].bitcast(U32).indirect(offs_t[:, (S - LAST) // STRIPE :]))
 
@@ -208,27 +210,21 @@ def tile_picked_lapl_silu_p_kernel(
             return h
 
         h_tiles = [project(0, 256, (3, 4, 5, 6))]
-        quantize_w1(*cast_w1(1, [0], None, nc.vector.tensor_copy))
-        quantize_w1(*cast_w1(1, [1], "w1_codes0_1", nc.scalar.copy))
+        quantize_w1(1, 0, nc.vector.tensor_copy)
+        quantize_w1(1, 1, nc.scalar.copy, "codes_w1_0_1")
+        quantize_w1_upper()
         h_tiles.append(project(1, BANK, (7, 0)))
-        quantize_w1(*cast_w1(2, [0, 1], "w1_codes0_1", nc.scalar.copy))
-        quantize_w1(*cast_w1(3, [0, 1], "w1_codes1_1", nc.scalar.copy))
         h_tiles.append(project(2, BANK, (1, 2)))
         h_tiles.append(project(3, BANK, (3, 4)))
 
-        z_bf = sbuf([P, V_BLOCKS, 2, P, 2], BF16, "z_bf", "w1_codes1_1")
+        z_bf = sbuf([P, V_BLOCKS, 2, P, 2], BF16, "z_bf")
 
-        reuse = {}
-        for n in range(D):
-            reuse[2, n, 3 * P] = "term3_%d_0" % (n + 1)
-            reuse[3, n, 3 * P] = "term3_%d_256" % (n + 1)
-
-        def laplacian(t, blocks, sum_bank):
+        def gather_terms(t, blocks):
             a, b = blocks[0] * P, (blocks[-1] + 1) * P
             cols = slice(a // STRIPE, b // STRIPE)
             terms = []
             for n in range(D + 1):
-                term = sbuf([P, b - a], F32, "term%d_%d_%d" % (t, n, a), reuse.get((t, n, a)))
+                term = sbuf([P, b - a], F32, "term%d_%d_%d" % (t, n, a))
                 if n < D:
                     nc.vector.tensor_tensor(
                         term[:], h_tiles[t][:].indirect(pos_t[n][:, cols]), signed_gates[n][:, a:b], MULT
@@ -236,43 +232,48 @@ def tile_picked_lapl_silu_p_kernel(
                 else:
                     nc.vector.tensor_tensor(term[:], h_tiles[t][:].indirect(cen_t[:, cols]), terms[0][:], SUBTRACT)
                 terms.append(term)
+            return {vb: [term[:, vb * P - a : (vb + 1) * P - a] for term in terms[1:]] for vb in blocks}
+
+        def sum_terms(t, terms, blocks, sum_bank):
+            a, b = blocks[0] * P, (blocks[-1] + 1) * P
             total = bank(sum_bank, "z_sum")
-            for n in range(1, D + 1):
-                for i in range(len(blocks)):
+            for n in range(D):
+                for i, vb in enumerate(blocks):
                     nc.tensor.matmul(
                         total[:, i * P : (i + 1) * P],
-                        lhsT=terms[n][:, i * P : (i + 1) * P],
+                        lhsT=terms[vb][n],
                         rhs=ident[:],
                         is_transpose=True,
-                        start=(n == 1 and i == 0),
-                        stop=(n == D and i == len(blocks) - 1),
+                        start=(n == 0 and i == 0),
+                        stop=(n == D - 1 and i == len(blocks) - 1),
                     )
-            nc.scalar.copy(
-                out=z_bf[:, blocks[0] : blocks[-1] + 1, :, QUAD * t : QUAD * (t + 1), :],
-                in_=total[:, 0 : b - a].rearrange("v (i m u e) -> v i u m e", m=QUAD, u=2, e=2),
-            )
+            rows = z_bf[:, blocks[0] : blocks[-1] + 1]
+            if t < 2:
+                nc.scalar.copy(
+                    out=rows[:, :, :, QUAD * t : QUAD * (t + 1), :],
+                    in_=total[:, 0 : b - a].rearrange("v (i m u e) -> v i u m e", m=QUAD, u=2, e=2),
+                )
+            else:
+                nc.scalar.copy(
+                    out=rows[:, :, t - 2, HALF:P, :], in_=total[:, 0 : b - a].rearrange("v (i m e) -> v i m e", m=HALF, e=2)
+                )
 
-        def turn_back(blocks, turn_bank):
-            first, width = blocks[0], len(blocks) * P
-            turned = bank(turn_bank, "turned")
+        def turn_back(turned, blocks, u):
             for i, vb in enumerate(blocks):
-                words = z_bf[:, vb].rearrange("v u m e -> v (u m e)").bitcast(F32)
-                for u in range(2):
-                    at = u * width + i * P
-                    nc.tensor.transpose(turned[:, at : at + P], words[:, u * P : (u + 1) * P], ident[:])
-            grouped = sbuf([P, width, 2], F32, "z_grouped%d" % first)
-            nc.scalar.copy(out=grouped[:], in_=turned[:, 0 : 2 * width].rearrange("m (u v) -> m v u", u=2))
-            return first, width, grouped
+                words = z_bf[:, vb, u].rearrange("v m e -> v (m e)").bitcast(F32)
+                at = (u * len(blocks) + i) * P
+                nc.tensor.transpose(turned[:, at : at + P], words, ident[:])
 
-        def quantize_z(first, width, grouped, codes_tag):
-            codes = sbuf([P, width], U32, "z_codes%d" % first, codes_tag)
-            plane = sbuf([P, width], U8, "z_plane%d" % first)
-            nc.vector.quantize_mx(
-                out=codes[:].bitcast(FP8X4),
-                scales=plane[:],
-                in_=grouped[:].rearrange("m v u -> m (v u)").bitcast(BF16),
-            )
-            return first * P, codes, plane
+        def interleave(turned, blocks):
+            width = len(blocks) * P
+            grouped = sbuf([P, width, 2], F32, "z_grouped%d" % blocks[0])
+            nc.scalar.copy(out=grouped[:], in_=turned[:, 0 : 2 * width].rearrange("m (u v) -> m v u", u=2))
+            return grouped
+
+        def quantize_z(grouped, blocks, codes_tag=None):
+            words = grouped[:].rearrange("m v u -> m (v u)").bitcast(BF16)
+            codes, plane = quantize(words, len(blocks) * P, "z%d" % blocks[0], codes_tag)
+            return blocks[0] * P, codes, plane
 
         def project_out(groups, out_bank, leave):
             first = groups[0][0]
@@ -292,15 +293,21 @@ def tile_picked_lapl_silu_p_kernel(
             leave(out=result[:], in_=acc[:, 0:end])
             nc.sync.dma_start(out=out[:, first : first + end], in_=result[:])
 
-        laplacian(0, [0, 1, 2, 3], 0)
-        laplacian(1, [0, 1, 2, 3], 4)
-        laplacian(2, [0, 1, 2], 3)
-        laplacian(3, [0, 1], 5)
-        turned = [turn_back([0, 1], 1)]
-        laplacian(3, [2], 6)
-        turned.append(turn_back([2], 2))
-        laplacian(2, [3], 1)
-        laplacian(3, [3], 2)
-        turned.append(turn_back([3], 3))
-        project_out([quantize_z(*turned[0], "term3_1_256"), quantize_z(*turned[1], None)], 2, nc.scalar.copy)
-        project_out([quantize_z(*turned[2], None)], 5, nc.vector.tensor_copy)
+        everyone = list(range(V_BLOCKS))
+        sum_terms(0, gather_terms(0, everyone), everyone, 0)
+        sum_terms(1, gather_terms(1, everyone), everyone, 2)
+        terms = gather_terms(2, everyone)
+        sum_terms(2, terms, [0, 1], 3)
+        sum_terms(2, terms, [2, 3], 4)
+        groups = [[0, 1], [2], [3]]
+        turned = [bank(n, "turned") for n in (1, 2, 7)]
+        for where, blocks in zip(turned, groups):
+            turn_back(where, blocks, 0)
+        grouped = []
+        for where, blocks, sum_bank in zip(turned, groups, (3, 4, 4)):
+            sum_terms(3, gather_terms(3, blocks), blocks, sum_bank)
+            turn_back(where, blocks, 1)
+            grouped.append(interleave(where, blocks))
+        early = [quantize_z(grouped[0], groups[0], "term3_0_384"), quantize_z(grouped[1], groups[1])]
+        project_out(early, 4, nc.scalar.copy)
+        project_out([quantize_z(grouped[2], groups[2])], 5, nc.vector.tensor_copy)

@@ -31,14 +31,13 @@ HALF = 64
 PLACES = {
     "w1_upper1": 0,
     "h1": 0,
-    "w1_raw1_0": 13312,
-    "term0_0_0": 13312,
-    "term0_1_0": 15360,
+    "term0_0_0": 15360,
     "w1_raw1_1": 16384,
-    "term0_2_0": 17408,
-    "w1_bf_upper": 19456,
+    "term0_1_0": 17408,
+    "term0_2_0": 19456,
     "x_window1": 24576,
     "w1_bf1_0": 24576,
+    "w1_bf1_1": 25600,
 }
 
 
@@ -155,17 +154,20 @@ def tile_picked_lapl_silu_p_kernel(
             nc.vector.quantize_mx(out=codes[:].bitcast(FP8X4), scales=plane[:], in_=grouped)
             return codes, plane
 
-        def quantize_w1(t, z, cast, staging_tag=None):
-            grouped = sbuf([P, P, PACK], BF16, "w1_bf%d_%d" % (t, z), staging_tag)
+        def cast_w1(t, z, cast):
+            grouped = sbuf([P, P, PACK], BF16, "w1_bf%d_%d" % (t, z))
             cast(
                 out=grouped[:].rearrange("p (c i) j -> p c j i", i=PACK),
                 in_=w1_raw[t, z].rearrange("p j (c i) -> p c j i", i=PACK),
             )
+            return grouped
+
+        def quantize_w1(t, z, grouped):
             codes, plane = quantize(grouped[:].rearrange("p c j -> p (c j)"), P, "w1_%d_%d" % (t, z))
             w1_mx[t, z] = (codes[:], plane[:])
 
         def quantize_w1_upper():
-            grouped = sbuf([P, 2, PASSES, HALF, 2, PACK], BF16, "w1_bf_upper")
+            grouped = sbuf([P, 2, PASSES, HALF, 2, PACK], BF16, "w1_bf_upper", "codes_w1_0_1")
             for z in range(PASSES):
                 nc.scalar.copy(
                     out=grouped[:, :, z].rearrange("p u m e j -> p u m j e"),
@@ -180,10 +182,10 @@ def tile_picked_lapl_silu_p_kernel(
         x_codes = [sbuf([P, S], U32, "x_codes0"), sbuf([P, S - LAST], U32, "x_codes1")]
 
         pick(x_codes[0], x_window[0][:].bitcast(U32), 0, S)
-        quantize_w1(0, 0, nc.scalar.copy)
+        quantize_w1(0, 0, cast_w1(0, 0, nc.scalar.copy))
         for a, b in [(0, 512), (512, S - LAST)]:
             pick(x_codes[1], x_window[1][:].bitcast(U32), a, b)
-        quantize_w1(0, 1, nc.scalar.copy)
+        quantize_w1(0, 1, cast_w1(0, 1, nc.scalar.copy))
         x_last = sbuf([P, LAST], U32, "x_last", "w1_raw0_1")
         nc.vector.tensor_copy(x_last[:], x_window[1][:].bitcast(U32).indirect(offs_t[:, (S - LAST) // STRIPE :]))
 
@@ -210,8 +212,9 @@ def tile_picked_lapl_silu_p_kernel(
             return h
 
         h_tiles = [project(0, 256, (3, 4, 5, 6))]
-        quantize_w1(1, 0, nc.vector.tensor_copy)
-        quantize_w1(1, 1, nc.scalar.copy, "codes_w1_0_1")
+        staged = [cast_w1(1, z, nc.vector.tensor_copy) for z in range(PASSES)]
+        for z in range(PASSES):
+            quantize_w1(1, z, staged[z])
         quantize_w1_upper()
         h_tiles.append(project(1, BANK, (7, 0)))
         h_tiles.append(project(2, BANK, (1, 2)))

@@ -35,6 +35,10 @@ PLACES = {
     "w1_raw1_1": 16384,
     "term0_1_0": 17408,
     "term0_2_0": 19456,
+    "plane_w1_0_1": 8192,
+    "signed_gate2": 8192,
+    "first_columns": 23552,
+    "w1_bf0_1": 23552,
     "x_window1": 24576,
     "w1_bf1_0": 24576,
     "w1_bf1_1": 25600,
@@ -131,20 +135,25 @@ def tile_picked_lapl_silu_p_kernel(
         upright = bank(7, "gate_upright")
         for d in range(D):
             nc.tensor.transpose(upright[:, d * P : (d + 1) * P], gate_rows[:, d, :], ident[:])
-        gate_columns = sbuf([P, D, V_BLOCKS], F32, "gate_columns")
-        nc.scalar.copy(
-            out=gate_columns[:], in_=upright[:, 0 : D * P].rearrange("n (d c) -> n d c", d=D)[:, :, 0:V_BLOCKS]
-        )
-        signed_gates = []
+        columns = upright[:, 0 : D * P].rearrange("n (d c) -> n d c", d=D)[:, :, 0:V_BLOCKS]
+        first_columns = sbuf([P, 1, V_BLOCKS], F32, "first_columns")
+        nc.scalar.copy(out=first_columns[:], in_=columns[:, 0:1])
+        other_columns = sbuf([P, D - 1, V_BLOCKS], F32, "other_columns")
+        nc.scalar.copy(out=other_columns[:], in_=columns[:, 1:D])
+        spreads = []
         for d in range(D):
             spread = bank(d, "gate_spread")
+            source = first_columns[:, 0] if d == 0 else other_columns[:, d - 1]
             for c in range(V_BLOCKS):
-                nc.tensor.transpose(
-                    spread[:, c * P : (c + 1) * P], gate_columns[:, d, c : c + 1].to_broadcast([P, P]), ident[:]
-                )
+                nc.tensor.transpose(spread[:, c * P : (c + 1) * P], source[:, c : c + 1].to_broadcast([P, P]), ident[:])
+            spreads.append(spread)
+
+        def sign_gate(d):
             tile = sbuf([P, V], F32, "signed_gate%d" % d)
-            nc.scalar.mul(out=tile[:], in_=spread[:], mul=1.0 if d == 0 else -1.0)
-            signed_gates.append(tile)
+            nc.scalar.mul(out=tile[:], in_=spreads[d][:], mul=1.0 if d == 0 else -1.0)
+            return tile
+
+        signed_gates = [sign_gate(0), sign_gate(1)]
 
         w1_mx = {}
 
@@ -212,6 +221,7 @@ def tile_picked_lapl_silu_p_kernel(
             return h
 
         h_tiles = [project(0, 256, (3, 4, 5, 6))]
+        signed_gates.append(sign_gate(2))
         staged = [cast_w1(1, z, nc.vector.tensor_copy) for z in range(PASSES)]
         for z in range(PASSES):
             quantize_w1(1, z, staged[z])

@@ -31,17 +31,21 @@ HALF = 64
 PLACES = {
     "w1_upper1": 0,
     "h1": 0,
-    "term0_0_0": 15360,
-    "w1_raw1_1": 16384,
-    "term0_1_0": 17408,
-    "term0_2_0": 19456,
+    "w1_raw1_0": 4096,
+    "term0_0_0": 4096,
     "plane_w1_0_1": 8192,
     "signed_gate2": 8192,
-    "first_columns": 23552,
-    "w1_bf0_1": 23552,
-    "x_window1": 24576,
-    "w1_bf1_0": 24576,
-    "w1_bf1_1": 25600,
+    "codes_w1_0_1": 12288,
+    "w1_bf1_1": 12288,
+    "term0_1_0": 15360,
+    "w1_raw1_1": 16384,
+    "term0_2_0": 17408,
+    "first_columns": 24576,
+    "w1_bf0_1": 24576,
+    "codes_w1_0_0": 26624,
+    "w1_bf_upper": 26624,
+    "x_window1": 32768,
+    "w1_bf1_0": 32768,
 }
 
 
@@ -113,9 +117,10 @@ def tile_picked_lapl_silu_p_kernel(
                 in_=picked_scales[q:QUAD:QUADS, 0:S].bitcast(I32),
             )
 
+        pos_t = [load_list(pos1, "pos_t0")]
         for z in range(PASSES):
-            w1_raw[1, z] = load_w1("w1_raw1_%d" % z, z, P, P, 1 + z)
-        pos_t = [load_list(source, "pos_t%d" % d) for d, source in enumerate((pos1, pos2, pos3))]
+            w1_raw[1, z] = load_w1("w1_raw1_%d" % z, z, P, P)
+        pos_t += [load_list(pos2, "pos_t1"), load_list(pos3, "pos_t2")]
         cen_t = load_list(cen, "cen_t")
         w1_upper = [load_w1("w1_upper%d" % z, z, 2 * P, 2 * P) for z in range(PASSES)]
         w2_codes = sbuf([P, N], I32, "w2_codes")
@@ -176,7 +181,7 @@ def tile_picked_lapl_silu_p_kernel(
             w1_mx[t, z] = (codes[:], plane[:])
 
         def quantize_w1_upper():
-            grouped = sbuf([P, 2, PASSES, HALF, 2, PACK], BF16, "w1_bf_upper", "codes_w1_0_1")
+            grouped = sbuf([P, 2, PASSES, HALF, 2, PACK], BF16, "w1_bf_upper", "w1_bf_upper")
             for z in range(PASSES):
                 nc.scalar.copy(
                     out=grouped[:, :, z].rearrange("p u m e j -> p u m j e"),
@@ -222,9 +227,8 @@ def tile_picked_lapl_silu_p_kernel(
 
         h_tiles = [project(0, 256, (3, 4, 5, 6))]
         signed_gates.append(sign_gate(2))
-        staged = [cast_w1(1, z, nc.vector.tensor_copy) for z in range(PASSES)]
-        for z in range(PASSES):
-            quantize_w1(1, z, staged[z])
+        for z, cast in enumerate((nc.vector.tensor_copy, nc.scalar.copy)):
+            quantize_w1(1, z, cast_w1(1, z, cast))
         quantize_w1_upper()
         h_tiles.append(project(1, BANK, (7, 0)))
         h_tiles.append(project(2, BANK, (1, 2)))

@@ -15,7 +15,6 @@ U8 = mybir.dt.uint8
 FP8X4 = mybir.dt.float8_e4m3fn_x4
 ACT = mybir.ActivationFunctionType
 MULT = mybir.AluOpType.mult
-SUBTRACT = mybir.AluOpType.subtract
 
 P = 128
 PACK = 4
@@ -29,21 +28,26 @@ QUAD = 32
 LAST = 256
 HALF = 64
 PLACES = {
-    "w1_upper1": 0,
-    "h1": 0,
-    "w1_raw1_0": 4096,
-    "term0_0_0": 4096,
-    "plane_w1_0_1": 8192,
-    "signed_gate2": 8192,
+    "w1_raw1_0": 0,
+    "term0_0_0": 0,
+    "w1_raw1_1": 8192,
+    "own0": 7168,
+    "signed_gate2": 9216,
+    "w1_upper1": 40960,
+    "z_bf": 40960,
     "codes_w1_0_1": 12288,
     "w1_bf1_1": 12288,
-    "term0_1_0": 15360,
-    "w1_raw1_1": 16384,
-    "term0_2_0": 17408,
+    "term0_1_0": 12288,
+    "codes_w1_1_1": 17408,
+    "w1_bf2": 17408,
+    "term1_1_0": 16384,
+    "term1_2_0": 18432,
+    "plane_w1_1_1": 20480,
+    "w1_bf3": 20480,
     "first_columns": 24576,
     "w1_bf0_1": 24576,
-    "codes_w1_0_0": 26624,
-    "w1_bf_upper": 26624,
+    "codes_w1_2": 26624,
+    "own1": 26624,
     "x_window1": 32768,
     "w1_bf1_0": 32768,
 }
@@ -118,10 +122,10 @@ def tile_picked_lapl_silu_p_kernel(
             )
 
         pos_t = [load_list(pos1, "pos_t0")]
+        cen_t = load_list(cen, "cen_t")
         for z in range(PASSES):
             w1_raw[1, z] = load_w1("w1_raw1_%d" % z, z, P, P)
         pos_t += [load_list(pos2, "pos_t1"), load_list(pos3, "pos_t2")]
-        cen_t = load_list(cen, "cen_t")
         w1_upper = [load_w1("w1_upper%d" % z, z, 2 * P, 2 * P) for z in range(PASSES)]
         w2_codes = sbuf([P, N], I32, "w2_codes")
         nc.sync.dma_start(out=w2_codes[:], in_=w2_words[0].rearrange("p n j -> p (n j)").bitcast(I32))
@@ -155,7 +159,7 @@ def tile_picked_lapl_silu_p_kernel(
 
         def sign_gate(d):
             tile = sbuf([P, V], F32, "signed_gate%d" % d)
-            nc.scalar.mul(out=tile[:], in_=spreads[d][:], mul=1.0 if d == 0 else -1.0)
+            nc.scalar.mul(out=tile[:], in_=spreads[d][:], mul=-1.0)
             return tile
 
         signed_gates = [sign_gate(0), sign_gate(1)]
@@ -180,18 +184,19 @@ def tile_picked_lapl_silu_p_kernel(
             codes, plane = quantize(grouped[:].rearrange("p c j -> p (c j)"), P, "w1_%d_%d" % (t, z))
             w1_mx[t, z] = (codes[:], plane[:])
 
-        def quantize_w1_upper():
-            grouped = sbuf([P, 2, PASSES, HALF, 2, PACK], BF16, "w1_bf_upper", "w1_bf_upper")
+        def cast_w1_upper(u):
+            grouped = sbuf([P, PASSES, HALF, 2, PACK], BF16, "w1_bf%d" % (2 + u))
             for z in range(PASSES):
                 nc.scalar.copy(
-                    out=grouped[:, :, z].rearrange("p u m e j -> p u m j e"),
-                    in_=w1_upper[z].rearrange("p j (m u e) -> p u m j e", u=2, e=2),
+                    out=grouped[:, z].rearrange("p m e j -> p m j e"),
+                    in_=w1_upper[z].rearrange("p j (m u e) -> p u m j e", u=2, e=2)[:, u],
                 )
-            codes, plane = quantize(grouped[:].rearrange("p u z m e j -> p (u z m e j)"), 2 * PASSES * P, "w1_upper")
-            for u in range(2):
-                for z in range(PASSES):
-                    at = (u * PASSES + z) * P
-                    w1_mx[2 + u, z] = (codes[:, at : at + P], plane[:, at : at + P])
+            return grouped
+
+        def quantize_w1_upper(u, grouped):
+            codes, plane = quantize(grouped[:].rearrange("p z m e j -> p (z m e j)"), PASSES * P, "w1_%d" % (2 + u))
+            for z in range(PASSES):
+                w1_mx[2 + u, z] = (codes[:, z * P : (z + 1) * P], plane[:, z * P : (z + 1) * P])
 
         x_codes = [sbuf([P, S], U32, "x_codes0"), sbuf([P, S - LAST], U32, "x_codes1")]
 
@@ -209,9 +214,11 @@ def tile_picked_lapl_silu_p_kernel(
         def project(t, width, banks):
             h = sbuf([P, S], F32, "h%d" % t)
             accs = [bank(n, "acc") for n in banks]
-            for z in range(PASSES):
-                codes, plane = w1_mx[t, z]
-                for a in range(0, S, LAST):
+            pieces = [(z, a) for z in range(PASSES) for a in range(0, S, LAST)]
+            if t > 0:
+                pieces = sorted(pieces, key=lambda piece: piece[1] // width)
+            for z, a in pieces:
+                    codes, plane = w1_mx[t, z]
                     nc.tensor.matmul_mx(
                         out=accs[a // width][:, a % width : a % width + LAST],
                         lhsT=codes.bitcast(FP8X4),
@@ -225,36 +232,33 @@ def tile_picked_lapl_silu_p_kernel(
                 nc.scalar.activation(out=h[:, i * width : (i + 1) * width], in_=acc[:, 0:width], func=ACT.Silu)
             return h
 
-        h_tiles = [project(0, 256, (3, 4, 5, 6))]
-        signed_gates.append(sign_gate(2))
-        for z, cast in enumerate((nc.vector.tensor_copy, nc.scalar.copy)):
-            quantize_w1(1, z, cast_w1(1, z, cast))
-        quantize_w1_upper()
-        h_tiles.append(project(1, BANK, (7, 0)))
-        h_tiles.append(project(2, BANK, (1, 2)))
-        h_tiles.append(project(3, BANK, (3, 4)))
-
         z_bf = sbuf([P, V_BLOCKS, 2, P, 2], BF16, "z_bf")
+        h_tiles = []
 
-        def gather_terms(t, blocks):
+        def gather_own(t):
+            own = sbuf([P, V], F32, "own%d" % t)
+            nc.scalar.activation(out=own[:], in_=h_tiles[t][:].indirect(cen_t[:]), func=ACT.Copy)
+            return own
+
+        def gather_neighbours(t, blocks):
             a, b = blocks[0] * P, (blocks[-1] + 1) * P
             cols = slice(a // STRIPE, b // STRIPE)
             terms = []
-            for n in range(D + 1):
+            for n in range(D):
                 term = sbuf([P, b - a], F32, "term%d_%d_%d" % (t, n, a))
-                if n < D:
-                    nc.vector.tensor_tensor(
-                        term[:], h_tiles[t][:].indirect(pos_t[n][:, cols]), signed_gates[n][:, a:b], MULT
-                    )
-                else:
-                    nc.vector.tensor_tensor(term[:], h_tiles[t][:].indirect(cen_t[:, cols]), terms[0][:], SUBTRACT)
+                nc.vector.tensor_tensor(
+                    term[:], h_tiles[t][:].indirect(pos_t[n][:, cols]), signed_gates[n][:, a:b], MULT
+                )
                 terms.append(term)
-            return {vb: [term[:, vb * P - a : (vb + 1) * P - a] for term in terms[1:]] for vb in blocks}
+            return {vb: [term[:, vb * P - a : (vb + 1) * P - a] for term in terms] for vb in blocks}
+
+        def with_own(terms, own, place):
+            return {vb: terms[vb][:place] + [own[:, vb * P : (vb + 1) * P]] + terms[vb][place:] for vb in terms}
 
         def sum_terms(t, terms, blocks, sum_bank):
             a, b = blocks[0] * P, (blocks[-1] + 1) * P
             total = bank(sum_bank, "z_sum")
-            for n in range(D):
+            for n in range(D + 1):
                 for i, vb in enumerate(blocks):
                     nc.tensor.matmul(
                         total[:, i * P : (i + 1) * P],
@@ -262,7 +266,7 @@ def tile_picked_lapl_silu_p_kernel(
                         rhs=ident[:],
                         is_transpose=True,
                         start=(n == 0 and i == 0),
-                        stop=(n == D - 1 and i == len(blocks) - 1),
+                        stop=(n == D and i == len(blocks) - 1),
                     )
             rows = z_bf[:, blocks[0] : blocks[-1] + 1]
             if t < 2:
@@ -311,9 +315,25 @@ def tile_picked_lapl_silu_p_kernel(
             nc.sync.dma_start(out=out[:, first : first + end], in_=result[:])
 
         everyone = list(range(V_BLOCKS))
-        sum_terms(0, gather_terms(0, everyone), everyone, 0)
-        sum_terms(1, gather_terms(1, everyone), everyone, 2)
-        terms = gather_terms(2, everyone)
+        h_tiles.append(project(0, 256, (3, 4, 5, 6)))
+        for z, cast in enumerate((nc.vector.tensor_copy, nc.scalar.copy)):
+            quantize_w1(1, z, cast_w1(1, z, cast))
+        signed_gates.append(sign_gate(2))
+        own = gather_own(0)
+        terms = gather_neighbours(0, everyone)
+        h_tiles.append(project(1, BANK, (7, 0)))
+        upper_bf = [cast_w1_upper(u) for u in range(2)]
+        sum_terms(0, with_own(terms, own, 1), everyone, 7)
+        for u in range(2):
+            quantize_w1_upper(u, upper_bf[u])
+        terms = gather_neighbours(1, everyone)
+        h_tiles.append(project(2, BANK, (1, 2)))
+        own = gather_own(1)
+        h_tiles.append(project(3, BANK, (3, 4)))
+        sum_terms(1, with_own(terms, own, D), everyone, 2)
+        terms = gather_neighbours(2, everyone)
+        terms = with_own(terms, gather_own(2), D)
+        own = gather_own(3)
         sum_terms(2, terms, [0, 1], 3)
         sum_terms(2, terms, [2, 3], 4)
         groups = [[0, 1], [2], [3]]
@@ -322,7 +342,7 @@ def tile_picked_lapl_silu_p_kernel(
             turn_back(where, blocks, 0)
         grouped = []
         for where, blocks, sum_bank in zip(turned, groups, (3, 4, 4)):
-            sum_terms(3, gather_terms(3, blocks), blocks, sum_bank)
+            sum_terms(3, with_own(gather_neighbours(3, blocks), own, 0), blocks, sum_bank)
             turn_back(where, blocks, 1)
             grouped.append(interleave(where, blocks))
         early = [quantize_z(grouped[0], groups[0], "term3_0_384"), quantize_z(grouped[1], groups[1])]

@@ -27,29 +27,46 @@ QUADS = 4
 QUAD = 32
 LAST = 256
 HALF = 64
+SPREAD = 2
 PLACES = {
     "w1_raw1_0": 0,
     "term0_0_0": 0,
-    "w1_raw1_1": 8192,
-    "own0": 7168,
-    "signed_gate2": 9216,
-    "w1_upper1": 40960,
-    "z_bf": 40960,
     "codes_w1_0_1": 12288,
     "w1_bf1_1": 12288,
     "term0_1_0": 12288,
     "codes_w1_1_1": 17408,
-    "w1_bf2": 17408,
+    "w1_bf_upper1": 17408,
     "term1_1_0": 16384,
     "term1_2_0": 18432,
-    "plane_w1_1_1": 20480,
-    "w1_bf3": 20480,
     "first_columns": 24576,
     "w1_bf0_1": 24576,
-    "codes_w1_2": 26624,
-    "own1": 26624,
     "x_window1": 32768,
     "w1_bf1_0": 32768,
+    "term2_0_0": 20480,
+    "term2_0_256": 20480,
+    "term2_1_0": 21504,
+    "term2_1_256": 21504,
+    "term2_2_0": 22528,
+    "term2_2_256": 22528,
+    "term3_0_384": 20480,
+    "term3_1_384": 21504,
+    "term3_2_384": 22528,
+    "codes_z0": 20480,
+    "term3_0_0": 26624,
+    "term3_0_256": 26624,
+    "term3_1_0": 27648,
+    "term3_1_256": 27648,
+    "term3_2_0": 28672,
+    "term3_2_256": 28672,
+    "own2_0": 30720,
+    "own2_256": 30720,
+    "own3_0": 31744,
+    "own3_256": 31744,
+    "w1_upper0": 40960,
+    "h1": 40960,
+    "w1_upper1": 49152,
+    "own0_0": 49152,
+    "own1_0": 51200,
 }
 
 
@@ -92,7 +109,7 @@ def tile_picked_lapl_silu_p_kernel(
         nc.vector.memset(scale_window[2 * QUAD : P, :].bitcast(I32), 0)
         x_plane = sbuf([P, S], U8, "x_plane")
         nc.vector.memset(x_plane[:].bitcast(I32), 0)
-        gate_rows = sbuf([P, D, P], F32, "gate_rows")
+        gate_rows = sbuf([P, SPREAD, P], F32, "gate_rows")
         nc.gpsimd.memset(gate_rows[:], 0.0)
         warm = sbuf([P, 2], F32, "warm")
         nc.vector.memset(warm[:, 0:1], 0.0)
@@ -104,7 +121,7 @@ def tile_picked_lapl_silu_p_kernel(
                 in_=x_scales[z].rearrange("(q r) n -> r q n", r=PACK).bitcast(I32),
             )
         offs_t = load_list(offs, "offs_t")
-        nc.sync.dma_start(out=gate_rows[0:V_BLOCKS], in_=gate[:, 0, :].rearrange("d (c n) -> c d n", n=P))
+        nc.sync.dma_start(out=gate_rows[0:V_BLOCKS], in_=gate[0:SPREAD, 0, :].rearrange("d (c n) -> c d n", n=P))
         x_window = [load_words(0)]
         w1_raw = {(0, 0): load_w1("w1_raw0_0", 0, 0, P)}
         x_window.append(load_words(1))
@@ -127,6 +144,8 @@ def tile_picked_lapl_silu_p_kernel(
             w1_raw[1, z] = load_w1("w1_raw1_%d" % z, z, P, P)
         pos_t += [load_list(pos2, "pos_t1"), load_list(pos3, "pos_t2")]
         w1_upper = [load_w1("w1_upper%d" % z, z, 2 * P, 2 * P) for z in range(PASSES)]
+        last_gate = sbuf([P, V], F32, "last_gate")
+        nc.sync.dma_start(out=last_gate[:], in_=gate[SPREAD])
         w2_codes = sbuf([P, N], I32, "w2_codes")
         nc.sync.dma_start(out=w2_codes[:], in_=w2_words[0].rearrange("p n j -> p (n j)").bitcast(I32))
         w2_plane = sbuf([P, N], U8, "w2_plane")
@@ -142,15 +161,15 @@ def tile_picked_lapl_silu_p_kernel(
         make_identity(nc, ident[:])
 
         upright = bank(7, "gate_upright")
-        for d in range(D):
+        for d in range(SPREAD):
             nc.tensor.transpose(upright[:, d * P : (d + 1) * P], gate_rows[:, d, :], ident[:])
-        columns = upright[:, 0 : D * P].rearrange("n (d c) -> n d c", d=D)[:, :, 0:V_BLOCKS]
+        columns = upright[:, 0 : SPREAD * P].rearrange("n (d c) -> n d c", d=SPREAD)[:, :, 0:V_BLOCKS]
         first_columns = sbuf([P, 1, V_BLOCKS], F32, "first_columns")
         nc.scalar.copy(out=first_columns[:], in_=columns[:, 0:1])
-        other_columns = sbuf([P, D - 1, V_BLOCKS], F32, "other_columns")
-        nc.scalar.copy(out=other_columns[:], in_=columns[:, 1:D])
+        other_columns = sbuf([P, SPREAD - 1, V_BLOCKS], F32, "other_columns")
+        nc.scalar.copy(out=other_columns[:], in_=columns[:, 1:SPREAD])
         spreads = []
-        for d in range(D):
+        for d in range(SPREAD):
             spread = bank(d, "gate_spread")
             source = first_columns[:, 0] if d == 0 else other_columns[:, d - 1]
             for c in range(V_BLOCKS):
@@ -159,15 +178,15 @@ def tile_picked_lapl_silu_p_kernel(
 
         def sign_gate(d):
             tile = sbuf([P, V], F32, "signed_gate%d" % d)
-            nc.scalar.mul(out=tile[:], in_=spreads[d][:], mul=-1.0)
+            nc.scalar.copy(out=tile[:], in_=spreads[d][:])
             return tile
 
-        signed_gates = [sign_gate(0), sign_gate(1)]
+        signed_gates = [sign_gate(0), sign_gate(1), last_gate]
 
         w1_mx = {}
 
-        def quantize(grouped, width, name, codes_tag=None):
-            codes = sbuf([P, width], U32, "codes_" + name, codes_tag)
+        def quantize(grouped, width, name):
+            codes = sbuf([P, width], U32, "codes_" + name)
             plane = sbuf([P, width], U8, "plane_" + name)
             nc.vector.quantize_mx(out=codes[:].bitcast(FP8X4), scales=plane[:], in_=grouped)
             return codes, plane
@@ -184,19 +203,18 @@ def tile_picked_lapl_silu_p_kernel(
             codes, plane = quantize(grouped[:].rearrange("p c j -> p (c j)"), P, "w1_%d_%d" % (t, z))
             w1_mx[t, z] = (codes[:], plane[:])
 
-        def cast_w1_upper(u):
-            grouped = sbuf([P, PASSES, HALF, 2, PACK], BF16, "w1_bf%d" % (2 + u))
-            for z in range(PASSES):
-                nc.scalar.copy(
-                    out=grouped[:, z].rearrange("p m e j -> p m j e"),
-                    in_=w1_upper[z].rearrange("p j (m u e) -> p u m j e", u=2, e=2)[:, u],
-                )
+        def cast_w1_upper(z):
+            grouped = sbuf([P, 2, HALF, 2, PACK], BF16, "w1_bf_upper%d" % z)
+            nc.scalar.copy(
+                out=grouped[:].rearrange("p u m e j -> p u m j e"),
+                in_=w1_upper[z].rearrange("p j (m u e) -> p u m j e", u=2, e=2),
+            )
             return grouped
 
-        def quantize_w1_upper(u, grouped):
-            codes, plane = quantize(grouped[:].rearrange("p z m e j -> p (z m e j)"), PASSES * P, "w1_%d" % (2 + u))
-            for z in range(PASSES):
-                w1_mx[2 + u, z] = (codes[:, z * P : (z + 1) * P], plane[:, z * P : (z + 1) * P])
+        def quantize_w1_upper(z, grouped):
+            codes, plane = quantize(grouped[:].rearrange("p u m e j -> p (u m e j)"), 2 * P, "w1_upper%d" % z)
+            for u in range(2):
+                w1_mx[2 + u, z] = (codes[:, u * P : (u + 1) * P], plane[:, u * P : (u + 1) * P])
 
         x_codes = [sbuf([P, S], U32, "x_codes0"), sbuf([P, S - LAST], U32, "x_codes1")]
 
@@ -215,8 +233,6 @@ def tile_picked_lapl_silu_p_kernel(
             h = sbuf([P, S], F32, "h%d" % t)
             accs = [bank(n, "acc") for n in banks]
             pieces = [(z, a) for z in range(PASSES) for a in range(0, S, LAST)]
-            if t > 0:
-                pieces = sorted(pieces, key=lambda piece: piece[1] // width)
             for z, a in pieces:
                     codes, plane = w1_mx[t, z]
                     nc.tensor.matmul_mx(
@@ -235,10 +251,12 @@ def tile_picked_lapl_silu_p_kernel(
         z_bf = sbuf([P, V_BLOCKS, 2, P, 2], BF16, "z_bf")
         h_tiles = []
 
-        def gather_own(t):
-            own = sbuf([P, V], F32, "own%d" % t)
-            nc.scalar.activation(out=own[:], in_=h_tiles[t][:].indirect(cen_t[:]), func=ACT.Copy)
-            return own
+        def gather_own(t, blocks):
+            a, b = blocks[0] * P, (blocks[-1] + 1) * P
+            own = sbuf([P, b - a], F32, "own%d_%d" % (t, a))
+            offsets = cen_t[:, a // STRIPE : b // STRIPE]
+            nc.scalar.activation(out=own[:], in_=h_tiles[t][:].indirect(offsets), func=ACT.Copy, scale=-1.0)
+            return {vb: own[:, vb * P - a : (vb + 1) * P - a] for vb in blocks}
 
         def gather_neighbours(t, blocks):
             a, b = blocks[0] * P, (blocks[-1] + 1) * P
@@ -253,7 +271,7 @@ def tile_picked_lapl_silu_p_kernel(
             return {vb: [term[:, vb * P - a : (vb + 1) * P - a] for term in terms] for vb in blocks}
 
         def with_own(terms, own, place):
-            return {vb: terms[vb][:place] + [own[:, vb * P : (vb + 1) * P]] + terms[vb][place:] for vb in terms}
+            return {vb: terms[vb][:place] + [own[vb]] + terms[vb][place:] for vb in terms}
 
         def sum_terms(t, terms, blocks, sum_bank):
             a, b = blocks[0] * P, (blocks[-1] + 1) * P
@@ -291,60 +309,61 @@ def tile_picked_lapl_silu_p_kernel(
             nc.scalar.copy(out=grouped[:], in_=turned[:, 0 : 2 * width].rearrange("m (u v) -> m v u", u=2))
             return grouped
 
-        def quantize_z(grouped, blocks, codes_tag=None):
+        def quantize_z(grouped, blocks):
             words = grouped[:].rearrange("m v u -> m (v u)").bitcast(BF16)
-            codes, plane = quantize(words, len(blocks) * P, "z%d" % blocks[0], codes_tag)
+            codes, plane = quantize(words, len(blocks) * P, "z%d" % blocks[0])
             return blocks[0] * P, codes, plane
 
-        def project_out(groups, out_bank, leave):
-            first = groups[0][0]
+        def project_out(group, out_bank, leave, result, first):
+            start, codes, plane = group
+            width = codes.shape[1]
             acc = bank(out_bank, "out_acc")
-            for start, codes, plane in groups:
-                end = start - first + codes.shape[1]
-                nc.tensor.matmul_mx(
-                    out=acc[:, start - first : end],
-                    lhsT=w2_codes[:].bitcast(FP8X4),
-                    lhsT_scale=w2_plane[:],
-                    rhs=codes[:].bitcast(FP8X4),
-                    rhs_scale=plane[:],
-                    start=True,
-                    stop=True,
-                )
-            result = sbuf([P, end], F32, "result%d" % first)
-            leave(out=result[:], in_=acc[:, 0:end])
-            nc.sync.dma_start(out=out[:, first : first + end], in_=result[:])
+            nc.tensor.matmul_mx(
+                out=acc[:, 0:width],
+                lhsT=w2_codes[:].bitcast(FP8X4),
+                lhsT_scale=w2_plane[:],
+                rhs=codes[:].bitcast(FP8X4),
+                rhs_scale=plane[:],
+                start=True,
+                stop=True,
+            )
+            leave(result[:, start - first : start - first + width], acc[:, 0:width], -1.0)
 
         everyone = list(range(V_BLOCKS))
         h_tiles.append(project(0, 256, (3, 4, 5, 6)))
         for z, cast in enumerate((nc.vector.tensor_copy, nc.scalar.copy)):
             quantize_w1(1, z, cast_w1(1, z, cast))
-        signed_gates.append(sign_gate(2))
-        own = gather_own(0)
-        terms = gather_neighbours(0, everyone)
+        quantize_w1_upper(0, cast_w1_upper(0))
+        terms = [gather_neighbours(0, everyone)]
         h_tiles.append(project(1, BANK, (7, 0)))
-        upper_bf = [cast_w1_upper(u) for u in range(2)]
-        sum_terms(0, with_own(terms, own, 1), everyone, 7)
-        for u in range(2):
-            quantize_w1_upper(u, upper_bf[u])
-        terms = gather_neighbours(1, everyone)
+        quantize_w1_upper(1, cast_w1_upper(1))
+        own = [gather_own(0, everyone), gather_own(1, everyone)]
+        terms.append(gather_neighbours(1, everyone))
         h_tiles.append(project(2, BANK, (1, 2)))
-        own = gather_own(1)
         h_tiles.append(project(3, BANK, (3, 4)))
-        sum_terms(1, with_own(terms, own, D), everyone, 2)
-        terms = gather_neighbours(2, everyone)
-        terms = with_own(terms, gather_own(2), D)
-        own = gather_own(3)
-        sum_terms(2, terms, [0, 1], 3)
-        sum_terms(2, terms, [2, 3], 4)
-        groups = [[0, 1], [2], [3]]
-        turned = [bank(n, "turned") for n in (1, 2, 7)]
-        for where, blocks in zip(turned, groups):
-            turn_back(where, blocks, 0)
+        early_own = [gather_own(2, [0, 1]), gather_own(3, [0, 1])]
+        sum_terms(0, with_own(terms[0], own[0], D), everyone, 7)
+        sum_terms(1, with_own(terms[1], own[1], 2), everyone, 0)
+        turned = {0: bank(1, "turned"), 2: bank(2, "turned"), 3: bank(7, "turned")}
         grouped = []
-        for where, blocks, sum_bank in zip(turned, groups, (3, 4, 4)):
-            sum_terms(3, with_own(gather_neighbours(3, blocks), own, 0), blocks, sum_bank)
-            turn_back(where, blocks, 1)
-            grouped.append(interleave(where, blocks))
-        early = [quantize_z(grouped[0], groups[0], "term3_0_384"), quantize_z(grouped[1], groups[1])]
-        project_out(early, 4, nc.scalar.copy)
-        project_out([quantize_z(grouped[2], groups[2])], 5, nc.vector.tensor_copy)
+        early, late = [0, 1], [2, 3]
+        sum_terms(2, with_own(gather_neighbours(2, early), early_own[0], 0), early, 5)
+        sum_terms(3, with_own(gather_neighbours(3, early), early_own[1], 0), early, 6)
+        for u in range(2):
+            turn_back(turned[0], early, u)
+        grouped.append(interleave(turned[0], early))
+        late_own = [gather_own(2, late), gather_own(3, late)]
+        sum_terms(2, with_own(gather_neighbours(2, late), late_own[0], 0), late, 3)
+        for vb in late:
+            turn_back(turned[vb], [vb], 0)
+        for vb, sum_bank in zip(late, (4, 5)):
+            sum_terms(3, with_own(gather_neighbours(3, [vb]), late_own[1], 0), [vb], sum_bank)
+            turn_back(turned[vb], [vb], 1)
+            grouped.append(interleave(turned[vb], [vb]))
+        groups = [[0, 1], [2], [3]]
+        results = [sbuf([P, 2 * P], F32, "result%d" % i) for i in range(2)]
+        project_out(quantize_z(grouped[0], groups[0]), 6, nc.vector.tensor_scalar_mul, results[0], 0)
+        nc.sync.dma_start(out=out[:, 0 : 2 * P], in_=results[0][:])
+        project_out(quantize_z(grouped[1], groups[1]), 7, nc.scalar.mul, results[1], 2 * P)
+        project_out(quantize_z(grouped[2], groups[2]), 0, nc.vector.tensor_scalar_mul, results[1], 2 * P)
+        nc.sync.dma_start(out=out[:, 2 * P : V], in_=results[1][:])

@@ -29,15 +29,11 @@ LAST = 256
 HALF = 64
 SPREAD = 2
 PLACES = {
-    "w1_raw1_0": 0,
-    "term0_0_0": 0,
+    "w1_raw1_1": 0,
+    "w1_bf_upper": 0,
     "codes_w1_0_1": 12288,
     "w1_bf1_1": 12288,
     "term0_1_0": 12288,
-    "codes_w1_1_1": 17408,
-    "w1_bf_upper1": 17408,
-    "term1_1_0": 16384,
-    "term1_2_0": 18432,
     "first_columns": 24576,
     "w1_bf0_1": 24576,
     "x_window1": 32768,
@@ -62,11 +58,9 @@ PLACES = {
     "own2_256": 30720,
     "own3_0": 31744,
     "own3_256": 31744,
-    "w1_upper0": 40960,
-    "h1": 40960,
     "w1_upper1": 49152,
-    "own0_0": 49152,
-    "own1_0": 51200,
+    "h1": 47104,
+    "own0_0": 51200,
 }
 
 
@@ -138,12 +132,13 @@ def tile_picked_lapl_silu_p_kernel(
                 in_=picked_scales[q:QUAD:QUADS, 0:S].bitcast(I32),
             )
 
+        rest = load_w1("w1_rest0", 0, P, H - P)
+        w1_raw[1, 0] = rest[:, :, 0:P]
         pos_t = [load_list(pos1, "pos_t0")]
-        cen_t = load_list(cen, "cen_t")
-        for z in range(PASSES):
-            w1_raw[1, z] = load_w1("w1_raw1_%d" % z, z, P, P)
+        w1_raw[1, 1] = load_w1("w1_raw1_1", 1, P, P)
         pos_t += [load_list(pos2, "pos_t1"), load_list(pos3, "pos_t2")]
-        w1_upper = [load_w1("w1_upper%d" % z, z, 2 * P, 2 * P) for z in range(PASSES)]
+        w1_upper = [rest[:, :, P : H - P], load_w1("w1_upper1", 1, 2 * P, 2 * P)]
+        cen_t = load_list(cen, "cen_t")
         last_gate = sbuf([P, V], F32, "last_gate")
         nc.sync.dma_start(out=last_gate[:], in_=gate[SPREAD])
         w2_codes = sbuf([P, N], I32, "w2_codes")
@@ -203,18 +198,18 @@ def tile_picked_lapl_silu_p_kernel(
             codes, plane = quantize(grouped[:].rearrange("p c j -> p (c j)"), P, "w1_%d_%d" % (t, z))
             w1_mx[t, z] = (codes[:], plane[:])
 
-        def cast_w1_upper(z):
-            grouped = sbuf([P, 2, HALF, 2, PACK], BF16, "w1_bf_upper%d" % z)
-            nc.scalar.copy(
-                out=grouped[:].rearrange("p u m e j -> p u m j e"),
-                in_=w1_upper[z].rearrange("p j (m u e) -> p u m j e", u=2, e=2),
-            )
-            return grouped
-
-        def quantize_w1_upper(z, grouped):
-            codes, plane = quantize(grouped[:].rearrange("p u m e j -> p (u m e j)"), 2 * P, "w1_upper%d" % z)
+        def quantize_w1_upper():
+            grouped = sbuf([P, 2, PASSES, HALF, 2, PACK], BF16, "w1_bf_upper")
+            for z in range(PASSES):
+                nc.scalar.copy(
+                    out=grouped[:, :, z].rearrange("p u m e j -> p u m j e"),
+                    in_=w1_upper[z].rearrange("p j (m u e) -> p u m j e", u=2, e=2),
+                )
+            codes, plane = quantize(grouped[:].rearrange("p u z m e j -> p (u z m e j)"), 2 * PASSES * P, "w1_upper")
             for u in range(2):
-                w1_mx[2 + u, z] = (codes[:, u * P : (u + 1) * P], plane[:, u * P : (u + 1) * P])
+                for z in range(PASSES):
+                    at = (u * PASSES + z) * P
+                    w1_mx[2 + u, z] = (codes[:, at : at + P], plane[:, at : at + P])
 
         x_codes = [sbuf([P, S], U32, "x_codes0"), sbuf([P, S - LAST], U32, "x_codes1")]
 
@@ -333,17 +328,16 @@ def tile_picked_lapl_silu_p_kernel(
         h_tiles.append(project(0, 256, (3, 4, 5, 6)))
         for z, cast in enumerate((nc.vector.tensor_copy, nc.scalar.copy)):
             quantize_w1(1, z, cast_w1(1, z, cast))
-        quantize_w1_upper(0, cast_w1_upper(0))
         terms = [gather_neighbours(0, everyone)]
+        quantize_w1_upper()
         h_tiles.append(project(1, BANK, (7, 0)))
-        quantize_w1_upper(1, cast_w1_upper(1))
         own = [gather_own(0, everyone), gather_own(1, everyone)]
         terms.append(gather_neighbours(1, everyone))
         h_tiles.append(project(2, BANK, (1, 2)))
         h_tiles.append(project(3, BANK, (3, 4)))
         early_own = [gather_own(2, [0, 1]), gather_own(3, [0, 1])]
-        sum_terms(0, with_own(terms[0], own[0], D), everyone, 7)
-        sum_terms(1, with_own(terms[1], own[1], 2), everyone, 0)
+        sum_terms(0, with_own(terms[0], own[0], D), everyone, 0)
+        sum_terms(1, with_own(terms[1], own[1], 2), everyone, 7)
         turned = {0: bank(1, "turned"), 2: bank(2, "turned"), 3: bank(7, "turned")}
         grouped = []
         early, late = [0, 1], [2, 3]

@@ -19,49 +19,16 @@ MULT = mybir.AluOpType.mult
 P = 128
 PACK = 4
 PASSES = K // (P * PACK)
-H_TILES = H // P
 V_BLOCKS = V // P
 BANK = 512
 STRIPE = 16
 QUADS = 4
 QUAD = 32
-LAST = 256
 HALF = 64
+WIDE = H // 2
 SPREAD = 2
-PLACES = {
-    "w1_raw1_1": 0,
-    "w1_bf_upper": 0,
-    "codes_w1_0_1": 12288,
-    "w1_bf1_1": 12288,
-    "term0_1_0": 12288,
-    "first_columns": 24576,
-    "w1_bf0_1": 24576,
-    "x_window1": 32768,
-    "w1_bf1_0": 32768,
-    "term2_0_0": 20480,
-    "term2_0_256": 20480,
-    "term2_1_0": 21504,
-    "term2_1_256": 21504,
-    "term2_2_0": 22528,
-    "term2_2_256": 22528,
-    "term3_0_384": 20480,
-    "term3_1_384": 21504,
-    "term3_2_384": 22528,
-    "codes_z0": 20480,
-    "term3_0_0": 26624,
-    "term3_0_256": 26624,
-    "term3_1_0": 27648,
-    "term3_1_256": 27648,
-    "term3_2_0": 28672,
-    "term3_2_256": 28672,
-    "own2_0": 30720,
-    "own2_256": 30720,
-    "own3_0": 31744,
-    "own3_256": 31744,
-    "w1_upper1": 49152,
-    "h1": 47104,
-    "own0_0": 51200,
-}
+LAST = 256
+ALIGN = 64
 
 
 def tile_picked_lapl_silu_p_kernel(
@@ -70,14 +37,24 @@ def tile_picked_lapl_silu_p_kernel(
     nc = tc.nc
     with ExitStack() as ctx:
         lists = ctx.enter_context(tc.tile_pool(name="lists", bufs=1))
-        keep = ctx.enter_context(tc.tile_pool(name="keep", bufs=1))
-        shared = ctx.enter_context(tc.tile_pool(name="shared", bufs=1))
+        work = ctx.enter_context(tc.tile_pool(name="work", bufs=1))
         psum = ctx.enter_context(tc.psum_pool(name="psum", bufs=1))
+        places = {"free": 0}
 
-        def sbuf(shape, dtype, name, tag=None):
-            if name in PLACES:
-                return shared.tile(shape, dtype, name=name, align_bytes=64, offset=PLACES[name])
-            return keep.tile(shape, dtype, name=name, tag=tag or name, align_bytes=64)
+        def sbuf(shape, dtype, name, over=None, shift=0, room=0):
+            if over is None:
+                size = 4 if dtype in (F32, I32, U32) else 2 if dtype == BF16 else 1
+                for extent in shape[1:]:
+                    size = size * extent
+                places[name] = places["free"]
+                places["free"] = places["free"] + -(-max(size, room) // ALIGN) * ALIGN
+            else:
+                places[name] = places[over] + shift
+            return work.tile(shape, dtype, name=name, align_bytes=ALIGN, offset=places[name])
+
+        def reserve(name, size):
+            places[name] = places["free"]
+            places["free"] = places["free"] + size
 
         def bank(n, name):
             return psum.tile([P, BANK], F32, name=name, tag="bank%d" % n)
@@ -92,12 +69,13 @@ def tile_picked_lapl_silu_p_kernel(
             nc.sync.dma_start(out=tile[:], in_=x_words[z].rearrange("p n j -> p (n j)").bitcast(I32))
             return tile
 
-        def load_w1(name, z, first, width, span=1):
-            tile = sbuf([P, span, PACK, width], F32, name)
+        def load_w1(name, z, first, width, over=None, shift=0, room=0):
+            tile = sbuf([P, PACK, width], F32, name, over, shift, room)
             rows = w1[z * P * PACK : (z + 1) * P * PACK, first : first + width]
-            nc.sync.dma_start(out=tile[:, 0], in_=rows.rearrange("(p j) c -> p j c", j=PACK))
-            return tile[:, 0]
+            nc.sync.dma_start(out=tile[:], in_=rows.rearrange("(p j) c -> p j c", j=PACK))
+            return tile
 
+        raw_bytes = 4 * PACK * WIDE
         scale_window = sbuf([P, T], U8, "scale_window")
         nc.vector.memset(scale_window[QUAD : 2 * QUAD, :].bitcast(I32), 0)
         nc.vector.memset(scale_window[2 * QUAD : P, :].bitcast(I32), 0)
@@ -117,15 +95,15 @@ def tile_picked_lapl_silu_p_kernel(
         offs_t = load_list(offs, "offs_t")
         nc.sync.dma_start(out=gate_rows[0:V_BLOCKS], in_=gate[0:SPREAD, 0, :].rearrange("d (c n) -> c d n", n=P))
         x_window = [load_words(0)]
-        w1_raw = {(0, 0): load_w1("w1_raw0_0", 0, 0, P)}
+        w1_raw = {(0, 0): load_w1("w1_raw0_0", 0, 0, P)[:]}
         x_window.append(load_words(1))
-        w1_raw[0, 1] = load_w1("w1_raw0_1", 1, 0, P)
+        w1_raw[0, 1] = load_w1("w1_raw0_1", 1, 0, P)[:]
 
         def pick(dst, window, a, b):
-            nc.vector.tensor_copy(dst[:, a:b], window.indirect(offs_t[:, a // STRIPE : b // STRIPE]))
+            nc.vector.tensor_copy(dst, window.indirect(offs_t[:, a // STRIPE : b // STRIPE]))
 
         picked_scales = sbuf([P, S], U8, "picked_scales")
-        pick(picked_scales, scale_window[:], 0, S)
+        pick(picked_scales[:], scale_window[:], 0, S)
         for q in range(QUADS):
             nc.sync.dma_start(
                 out=x_plane[QUAD * q : QUAD * q + PASSES * PACK, :].bitcast(I32),
@@ -134,10 +112,12 @@ def tile_picked_lapl_silu_p_kernel(
 
         rest = load_w1("w1_rest0", 0, P, H - P)
         w1_raw[1, 0] = rest[:, :, 0:P]
+        w1_upper = [rest[:, :, P : H - P]]
+        w1_raw[1, 1] = load_w1("w1_raw1_1", 1, P, P)[:]
         pos_t = [load_list(pos1, "pos_t0")]
-        w1_raw[1, 1] = load_w1("w1_raw1_1", 1, P, P)
-        pos_t += [load_list(pos2, "pos_t1"), load_list(pos3, "pos_t2")]
-        w1_upper = [rest[:, :, P : H - P], load_w1("w1_upper1", 1, 2 * P, 2 * P)]
+        pos_t.append(load_list(pos2, "pos_t1"))
+        w1_upper.append(load_w1("w1_upper1", 1, WIDE, WIDE)[:])
+        pos_t.append(load_list(pos3, "pos_t2"))
         cen_t = load_list(cen, "cen_t")
         last_gate = sbuf([P, V], F32, "last_gate")
         nc.sync.dma_start(out=last_gate[:], in_=gate[SPREAD])
@@ -151,162 +131,209 @@ def tile_picked_lapl_silu_p_kernel(
                 in_=w2_scales[0, PACK * q : PACK * (q + 1), :].bitcast(I32),
             )
 
-
         ident = sbuf([P, P], F32, "ident")
         make_identity(nc, ident[:])
 
         upright = bank(7, "gate_upright")
         for d in range(SPREAD):
             nc.tensor.transpose(upright[:, d * P : (d + 1) * P], gate_rows[:, d, :], ident[:])
-        columns = upright[:, 0 : SPREAD * P].rearrange("n (d c) -> n d c", d=SPREAD)[:, :, 0:V_BLOCKS]
-        first_columns = sbuf([P, 1, V_BLOCKS], F32, "first_columns")
-        nc.scalar.copy(out=first_columns[:], in_=columns[:, 0:1])
-        other_columns = sbuf([P, SPREAD - 1, V_BLOCKS], F32, "other_columns")
-        nc.scalar.copy(out=other_columns[:], in_=columns[:, 1:SPREAD])
+        upright_columns = upright[:, 0 : SPREAD * P].rearrange("n (d c) -> n d c", d=SPREAD)
+        columns = []
+        for d in range(SPREAD):
+            tile = sbuf([P, V_BLOCKS], F32, "gate_columns%d" % d, room=2 * P * PACK)
+            nc.scalar.copy(out=tile[:], in_=upright_columns[:, d, 0:V_BLOCKS])
+            columns.append(tile)
         spreads = []
         for d in range(SPREAD):
             spread = bank(d, "gate_spread")
-            source = first_columns[:, 0] if d == 0 else other_columns[:, d - 1]
             for c in range(V_BLOCKS):
-                nc.tensor.transpose(spread[:, c * P : (c + 1) * P], source[:, c : c + 1].to_broadcast([P, P]), ident[:])
+                nc.tensor.transpose(
+                    spread[:, c * P : (c + 1) * P], columns[d][:, c : c + 1].to_broadcast([P, P]), ident[:]
+                )
             spreads.append(spread)
-
-        def sign_gate(d):
-            tile = sbuf([P, V], F32, "signed_gate%d" % d)
+        gates = []
+        for d in range(SPREAD):
+            tile = sbuf([P, V], F32, "gate%d" % d)
             nc.scalar.copy(out=tile[:], in_=spreads[d][:])
-            return tile
-
-        signed_gates = [sign_gate(0), sign_gate(1), last_gate]
+            gates.append(tile)
+        gates.append(last_gate)
 
         w1_mx = {}
 
-        def quantize(grouped, width, name):
-            codes = sbuf([P, width], U32, "codes_" + name)
-            plane = sbuf([P, width], U8, "plane_" + name)
+        def quantize(grouped, width, name, room=0, over=None):
+            codes = sbuf([P, width], U32, "codes_" + name, over, room=room)
+            plane = sbuf([P, width], U8, "plane_" + name, room=room)
             nc.vector.quantize_mx(out=codes[:].bitcast(FP8X4), scales=plane[:], in_=grouped)
             return codes, plane
 
-        def cast_w1(t, z, cast):
-            grouped = sbuf([P, P, PACK], BF16, "w1_bf%d_%d" % (t, z))
+        def cast_tile(grouped, t, z, cast=nc.scalar.copy):
             cast(
-                out=grouped[:].rearrange("p (c i) j -> p c j i", i=PACK),
+                out=grouped.rearrange("p m e j -> p (m e) j").rearrange("p (c i) j -> p c j i", i=PACK),
                 in_=w1_raw[t, z].rearrange("p j (c i) -> p c j i", i=PACK),
             )
-            return grouped
 
-        def quantize_w1(t, z, grouped):
-            codes, plane = quantize(grouped[:].rearrange("p c j -> p (c j)"), P, "w1_%d_%d" % (t, z))
-            w1_mx[t, z] = (codes[:], plane[:])
+        def staging(name, count, over=None, shift=0):
+            return sbuf([P, count, HALF, 2, PACK], BF16, name, over, shift)
 
-        def quantize_w1_upper():
-            grouped = sbuf([P, 2, PASSES, HALF, 2, PACK], BF16, "w1_bf_upper")
-            for z in range(PASSES):
-                nc.scalar.copy(
-                    out=grouped[:, :, z].rearrange("p u m e j -> p u m j e"),
-                    in_=w1_upper[z].rearrange("p j (m u e) -> p u m j e", u=2, e=2),
-                )
-            codes, plane = quantize(grouped[:].rearrange("p u z m e j -> p (u z m e j)"), 2 * PASSES * P, "w1_upper")
-            for u in range(2):
-                for z in range(PASSES):
-                    at = (u * PASSES + z) * P
-                    w1_mx[2 + u, z] = (codes[:, at : at + P], plane[:, at : at + P])
+        def quantize_w1(grouped, keys, name, room=0, over=None):
+            codes, plane = quantize(grouped.rearrange("p n m e j -> p (n m e j)"), len(keys) * P, name, room, over)
+            for n, key in enumerate(keys):
+                w1_mx[key] = (codes[:, n * P : (n + 1) * P], plane[:, n * P : (n + 1) * P])
 
-        x_codes = [sbuf([P, S], U32, "x_codes0"), sbuf([P, S - LAST], U32, "x_codes1")]
-
-        pick(x_codes[0], x_window[0][:].bitcast(U32), 0, S)
-        quantize_w1(0, 0, cast_w1(0, 0, nc.scalar.copy))
-        for a, b in [(0, 512), (512, S - LAST)]:
-            pick(x_codes[1], x_window[1][:].bitcast(U32), a, b)
-        quantize_w1(0, 1, cast_w1(0, 1, nc.scalar.copy))
-        x_last = sbuf([P, LAST], U32, "x_last", "w1_raw0_1")
-        nc.vector.tensor_copy(x_last[:], x_window[1][:].bitcast(U32).indirect(offs_t[:, (S - LAST) // STRIPE :]))
+        x_codes = [sbuf([P, S], U32, "x_codes0")]
+        pick(x_codes[0][:], x_window[0][:].bitcast(U32), 0, S)
+        first = staging("w1_bf0_0", 1)
+        cast_tile(first[:, 0], 0, 0)
+        quantize_w1(first[:], [(0, 0)], "w1_0_0")
+        x_codes.append(sbuf([P, S - LAST], U32, "x_codes1"))
+        for a, b in [(0, BANK), (BANK, S - LAST)]:
+            pick(x_codes[1][:, a:b], x_window[1][:].bitcast(U32), a, b)
+        second = staging("w1_bf0_1", 1, "gate_columns0")
+        cast_tile(second[:, 0], 0, 1)
+        quantize_w1(second[:], [(0, 1)], "w1_0_1", 4 * WIDE * PACK)
+        x_last = sbuf([P, LAST], U32, "x_last", over="w1_raw0_1")
+        pick(x_last[:], x_window[1][:].bitcast(U32), S - LAST, S)
+        for z in range(PASSES):
+            grouped = staging("w1_bf1_%d" % z, 1)
+            cast_tile(grouped[:, 0], 1, z, nc.vector.tensor_copy)
+            quantize_w1(grouped[:], [(1, z)], "w1_1_%d" % z)
 
         def picked_words(z, a, b):
             return x_last[:] if (z, a) == (1, S - LAST) else x_codes[z][:, a:b]
 
-        def project(t, width, banks):
-            h = sbuf([P, S], F32, "h%d" % t)
-            accs = [bank(n, "acc") for n in banks]
-            pieces = [(z, a) for z in range(PASSES) for a in range(0, S, LAST)]
-            for z, a in pieces:
-                    codes, plane = w1_mx[t, z]
+        def multiply(t, z, accs, cuts):
+            codes, plane = w1_mx[t, z]
+            for acc, (first, last) in zip(accs, cuts):
+                stops = [first, S - LAST, last] if z == 1 and first < S - LAST < last else [first, last]
+                for a, b in zip(stops, stops[1:]):
                     nc.tensor.matmul_mx(
-                        out=accs[a // width][:, a % width : a % width + LAST],
+                        out=acc[:, a - first : b - first],
                         lhsT=codes.bitcast(FP8X4),
                         lhsT_scale=plane,
-                        rhs=picked_words(z, a, a + LAST).bitcast(FP8X4),
-                        rhs_scale=x_plane[PACK * z : P, a : a + LAST],
-                        start=(z == 0 and a % width == 0),
-                        stop=(z == PASSES - 1 and (a + LAST) % width == 0),
+                        rhs=picked_words(z, a, b).bitcast(FP8X4),
+                        rhs_scale=x_plane[PACK * z : P, a:b],
+                        start=(z == 0),
+                        stop=(z == PASSES - 1 and b == last),
                     )
-            for i, acc in enumerate(accs):
-                nc.scalar.activation(out=h[:, i * width : (i + 1) * width], in_=acc[:, 0:width], func=ACT.Silu)
-            return h
 
-        z_bf = sbuf([P, V_BLOCKS, 2, P, 2], BF16, "z_bf")
-        h_tiles = []
+        h_tiles = {}
 
-        def gather_own(t, blocks):
-            a, b = blocks[0] * P, (blocks[-1] + 1) * P
-            own = sbuf([P, b - a], F32, "own%d_%d" % (t, a))
-            offsets = cen_t[:, a // STRIPE : b // STRIPE]
-            nc.scalar.activation(out=own[:], in_=h_tiles[t][:].indirect(offsets), func=ACT.Copy, scale=-1.0)
-            return {vb: own[:, vb * P - a : (vb + 1) * P - a] for vb in blocks}
+        def activate(t, accs, cuts, over=None):
+            h = sbuf([P, S], F32, "h%d" % t, over)
+            for acc, (first, last) in zip(accs, cuts):
+                nc.scalar.activation(out=h[:, first:last], in_=acc[:, 0 : last - first], func=ACT.Silu)
+            h_tiles[t] = h
 
-        def gather_neighbours(t, blocks):
-            a, b = blocks[0] * P, (blocks[-1] + 1) * P
-            cols = slice(a // STRIPE, b // STRIPE)
-            terms = []
-            for n in range(D):
-                term = sbuf([P, b - a], F32, "term%d_%d_%d" % (t, n, a))
-                nc.vector.tensor_tensor(
-                    term[:], h_tiles[t][:].indirect(pos_t[n][:, cols]), signed_gates[n][:, a:b], MULT
-                )
-                terms.append(term)
-            return {vb: [term[:, vb * P - a : (vb + 1) * P - a] for term in terms] for vb in blocks}
+        first_cuts = [(a, a + LAST) for a in range(0, S, LAST)]
+        cuts = [(0, BANK), (BANK, S)]
+        accs = {0: [bank(n, "acc0") for n in (2, 3, 4, 5)], 1: [bank(n, "acc1") for n in (6, 7)]}
+        for z in range(PASSES):
+            multiply(0, z, accs[0], first_cuts)
+        activate(0, accs[0], first_cuts)
+        for z in range(PASSES):
+            multiply(1, z, accs[1], cuts)
 
-        def with_own(terms, own, place):
-            return {vb: terms[vb][:place] + [own[vb]] + terms[vb][place:] for vb in terms}
+        upper = staging("w1_bf_upper", 2 * PASSES, "codes_w1_0_1")
 
-        def sum_terms(t, terms, blocks, sum_bank):
-            a, b = blocks[0] * P, (blocks[-1] + 1) * P
+        def cast_upper(z):
+            nc.scalar.copy(
+                out=upper[:, 2 * z : 2 * z + 2].rearrange("p u m e j -> p m j u e"),
+                in_=w1_upper[z].rearrange("p j (m u e) -> p m j u e", u=2, e=2),
+            )
+
+        cast_upper(0)
+        activate(1, accs[1], cuts, "w1_rest0")
+        accs[2] = [bank(n, "acc2") for n in (0, 1)]
+        accs[3] = [bank(n, "acc3") for n in (2, 3)]
+
+        def gather_gated(t, n, a, b, over=None, shift=0):
+            term = sbuf([P, b - a], F32, "term%d_%d_%d" % (t, n, a), over, shift)
+            offsets = pos_t[n][:, a // STRIPE : b // STRIPE]
+            nc.vector.tensor_tensor(term[:], h_tiles[t][:].indirect(offsets), gates[n][:, a:b], MULT)
+            return term
+
+        def gather_plain(t, offsets, a, b, name, scale, over=None, shift=0, room=0):
+            values = sbuf([P, b - a], F32, name, over, shift, room)
+            nc.scalar.activation(
+                out=values[:], in_=h_tiles[t][:].indirect(offsets[:, a // STRIPE : b // STRIPE]), func=ACT.Copy, scale=scale
+            )
+            return values
+
+        def gate_plain(t, n, a, b, values):
+            term = sbuf([P, b - a], F32, "term%d_%d_%d" % (t, n, a))
+            nc.vector.tensor_tensor(term[:], values[:], gates[n][:, a:b], MULT)
+            return term
+
+        half_bytes = 4 * V
+        mid = V // 2
+        terms0 = [gather_gated(0, 0, 0, V, "w1_raw1_1"), gather_gated(0, 1, 0, V)]
+        quantize_w1(upper[:, 0:1], [(2, 0)], "w1_2_0", over="codes_w1_1_1")
+        multiply(2, 0, accs[2], cuts)
+        terms1 = [gather_gated(1, 0, 0, V)]
+        cast_upper(1)
+        quantize_w1(upper[:, 1:], [(3, 0), (2, 1), (3, 1)], "w1_rest")
+        for t, z in [(2, 1), (3, 0), (3, 1)]:
+            multiply(t, z, accs[t], cuts)
+        plain0 = gather_plain(0, pos_t[2], 0, V, "plain0", 1.0, room=4 * (mid + V))
+        terms1.append(gather_gated(1, 1, 0, V, "w1_upper1", 0))
+        terms0.append(gate_plain(0, 2, 0, V, plain0))
+        terms1.append(gather_gated(1, 2, 0, V, "w1_upper1", half_bytes))
+        halves = [gather_plain(0, cen_t, 0, mid, "own0_early", -1.0)]
+        activate(2, accs[2], cuts)
+        halves.append(gather_plain(0, cen_t, mid, V, "own0_late", -1.0, "plain0"))
+        own = {1: gather_plain(1, cen_t, 0, V, "own1", -1.0, "plain0", 4 * mid)}
+        activate(3, accs[3], cuts)
+        for t in (2, 3):
+            own[t] = gather_plain(t, cen_t, 0, V, "own%d" % t, -1.0)
+
+        everyone, early, late = list(range(V_BLOCKS)), [0, 1], [2, 3]
+        groups = [early, [2], [3]]
+        z_bf = {group[0]: sbuf([P, len(group), 2, P, 2], BF16, "z_bf%d" % group[0]) for group in groups}
+
+        def columns_of(tile, first, blocks):
+            return [tile[:, vb * P - first : (vb + 1) * P - first] for vb in blocks]
+
+        def sum_terms(parts, blocks, sum_bank):
             total = bank(sum_bank, "z_sum")
-            for n in range(D + 1):
-                for i, vb in enumerate(blocks):
+            for n, part in enumerate(parts):
+                for i, piece in enumerate(part):
                     nc.tensor.matmul(
                         total[:, i * P : (i + 1) * P],
-                        lhsT=terms[vb][n],
+                        lhsT=piece,
                         rhs=ident[:],
                         is_transpose=True,
                         start=(n == 0 and i == 0),
-                        stop=(n == D and i == len(blocks) - 1),
+                        stop=(n == len(parts) - 1 and i == len(blocks) - 1),
                     )
-            rows = z_bf[:, blocks[0] : blocks[-1] + 1]
+            return {vb: (total, i * P) for i, vb in enumerate(blocks)}
+
+        def round_off(t, totals, blocks):
+            total, at = totals[blocks[0]]
+            sums = total[:, at : at + len(blocks) * P]
+            rows = z_bf[blocks[0]]
             if t < 2:
                 nc.scalar.copy(
                     out=rows[:, :, :, QUAD * t : QUAD * (t + 1), :],
-                    in_=total[:, 0 : b - a].rearrange("v (i m u e) -> v i u m e", m=QUAD, u=2, e=2),
+                    in_=sums.rearrange("v (i m u e) -> v i u m e", m=QUAD, u=2, e=2),
                 )
             else:
-                nc.scalar.copy(
-                    out=rows[:, :, t - 2, HALF:P, :], in_=total[:, 0 : b - a].rearrange("v (i m e) -> v i m e", m=HALF, e=2)
-                )
+                nc.scalar.copy(out=rows[:, :, t - 2, HALF:P, :], in_=sums.rearrange("v (i m e) -> v i m e", m=HALF, e=2))
 
         def turn_back(turned, blocks, u):
-            for i, vb in enumerate(blocks):
-                words = z_bf[:, vb, u].rearrange("v m e -> v (m e)").bitcast(F32)
+            for i in range(len(blocks)):
+                words = z_bf[blocks[0]][:, i, u].rearrange("v m e -> v (m e)").bitcast(F32)
                 at = (u * len(blocks) + i) * P
                 nc.tensor.transpose(turned[:, at : at + P], words, ident[:])
 
-        def interleave(turned, blocks):
+        def interleave(turned, blocks, move=nc.scalar.copy, over=None):
             width = len(blocks) * P
-            grouped = sbuf([P, width, 2], F32, "z_grouped%d" % blocks[0])
-            nc.scalar.copy(out=grouped[:], in_=turned[:, 0 : 2 * width].rearrange("m (u v) -> m v u", u=2))
+            grouped = sbuf([P, width, 2], F32, "z_grouped%d" % blocks[0], over)
+            move(out=grouped[:], in_=turned[:, 0 : 2 * width].rearrange("m (u v) -> m v u", u=2))
             return grouped
 
-        def quantize_z(grouped, blocks):
+        def quantize_z(grouped, blocks, over=None):
             words = grouped[:].rearrange("m v u -> m (v u)").bitcast(BF16)
-            codes, plane = quantize(words, len(blocks) * P, "z%d" % blocks[0])
+            codes, plane = quantize(words, len(blocks) * P, "z%d" % blocks[0], over=over)
             return blocks[0] * P, codes, plane
 
         def project_out(group, out_bank, leave, result, first):
@@ -324,40 +351,41 @@ def tile_picked_lapl_silu_p_kernel(
             )
             leave(result[:, start - first : start - first + width], acc[:, 0:width], -1.0)
 
-        everyone = list(range(V_BLOCKS))
-        h_tiles.append(project(0, 256, (3, 4, 5, 6)))
-        for z, cast in enumerate((nc.vector.tensor_copy, nc.scalar.copy)):
-            quantize_w1(1, z, cast_w1(1, z, cast))
-        terms = [gather_neighbours(0, everyone)]
-        quantize_w1_upper()
-        h_tiles.append(project(1, BANK, (7, 0)))
-        own = [gather_own(0, everyone), gather_own(1, everyone)]
-        terms.append(gather_neighbours(1, everyone))
-        h_tiles.append(project(2, BANK, (1, 2)))
-        h_tiles.append(project(3, BANK, (3, 4)))
-        early_own = [gather_own(2, [0, 1]), gather_own(3, [0, 1])]
-        sum_terms(0, with_own(terms[0], own[0], D), everyone, 0)
-        sum_terms(1, with_own(terms[1], own[1], 2), everyone, 7)
-        turned = {0: bank(1, "turned"), 2: bank(2, "turned"), 3: bank(7, "turned")}
-        grouped = []
-        early, late = [0, 1], [2, 3]
-        sum_terms(2, with_own(gather_neighbours(2, early), early_own[0], 0), early, 5)
-        sum_terms(3, with_own(gather_neighbours(3, early), early_own[1], 0), early, 6)
-        for u in range(2):
-            turn_back(turned[0], early, u)
-        grouped.append(interleave(turned[0], early))
-        late_own = [gather_own(2, late), gather_own(3, late)]
-        sum_terms(2, with_own(gather_neighbours(2, late), late_own[0], 0), late, 3)
-        for vb in late:
-            turn_back(turned[vb], [vb], 0)
-        for vb, sum_bank in zip(late, (4, 5)):
-            sum_terms(3, with_own(gather_neighbours(3, [vb]), late_own[1], 0), [vb], sum_bank)
-            turn_back(turned[vb], [vb], 1)
-            grouped.append(interleave(turned[vb], [vb]))
-        groups = [[0, 1], [2], [3]]
+        first_own = columns_of(halves[0], 0, early) + columns_of(halves[1], mid, late)
+        totals = [
+            sum_terms([columns_of(x, 0, everyone) for x in terms0] + [first_own], everyone, 4),
+            sum_terms([columns_of(x, 0, everyone) for x in terms1 + [own[1]]], everyone, 1),
+        ]
+        terms = [gather_gated(2, n, 0, V) for n in range(D)]
+        totals.append(sum_terms([columns_of(x, 0, everyone) for x in terms + [own[2]]], everyone, 6))
+        terms = [gather_gated(3, n, 0, mid) for n in range(D)]
+        totals.append(sum_terms([columns_of(x, 0, early) for x in terms + [own[3]]], early, 7))
+        turned = [bank(2, "turned")]
+        for t in range(3):
+            round_off(t, totals[t], early)
+        turn_back(turned[0], early, 0)
+        for t in (2, 0):
+            for group in groups[1:]:
+                round_off(t, totals[t], group)
+        round_off(3, totals[3], early)
+        turn_back(turned[0], early, 1)
+        for group in groups[1:]:
+            round_off(1, totals[1], group)
+        last_totals = {}
+        for vb, sum_bank in zip(late, (6, 7)):
+            terms = [gather_gated(3, n, vb * P, (vb + 1) * P) for n in range(D)]
+            last_totals[vb] = sum_terms([columns_of(own[3], 0, [vb])] + [[x[:]] for x in terms], [vb], sum_bank)
+        turned += [bank(0, "turned"), bank(5, "turned")]
+        for g in (1, 2):
+            turn_back(turned[g], groups[g], 0)
+        grouped = [interleave(turned[0], early, nc.vector.tensor_copy, "h3")]
+        for g in (1, 2):
+            round_off(3, last_totals[groups[g][0]], groups[g])
+            turn_back(turned[g], groups[g], 1)
+        grouped += [interleave(turned[g], groups[g]) for g in (1, 2)]
         results = [sbuf([P, 2 * P], F32, "result%d" % i) for i in range(2)]
-        project_out(quantize_z(grouped[0], groups[0]), 6, nc.vector.tensor_scalar_mul, results[0], 0)
+        project_out(quantize_z(grouped[0], groups[0]), 3, nc.vector.tensor_scalar_mul, results[0], 0)
         nc.sync.dma_start(out=out[:, 0 : 2 * P], in_=results[0][:])
-        project_out(quantize_z(grouped[1], groups[1]), 7, nc.scalar.mul, results[1], 2 * P)
-        project_out(quantize_z(grouped[2], groups[2]), 0, nc.vector.tensor_scalar_mul, results[1], 2 * P)
+        project_out(quantize_z(grouped[1], groups[1]), 5, nc.scalar.mul, results[1], 2 * P)
+        project_out(quantize_z(grouped[2], groups[2]), 4, nc.vector.tensor_scalar_mul, results[1], 2 * P)
         nc.sync.dma_start(out=out[:, 2 * P : V], in_=results[1][:])

from contextlib import ExitStack

import concourse.mybir as mybir
from concourse.masks import make_identity

K, T, S, D, V, H, N = 1024, 2048, 1024, 3, 512, 512, 128
FLOPS = 2 * K * H * S + 2 * H * N * V

F32 = mybir.dt.float32
BF16 = mybir.dt.bfloat16
I32 = mybir.dt.int32
U32 = mybir.dt.uint32
U16 = mybir.dt.uint16
U8 = mybir.dt.uint8
FP8X4 = mybir.dt.float8_e4m3fn_x4
ACT = mybir.ActivationFunctionType
MULT = mybir.AluOpType.mult

P = 128
PACK = 4
PASSES = K // (P * PACK)
V_BLOCKS = V // P
BANK = 512
STRIPE = 16
QUADS = 4
QUAD = 32
HALF = 64
WIDE = H // 2
SPREAD = 2
LAST = 256
ALIGN = 64


def tile_picked_lapl_silu_p_kernel(
    tc, x_words, x_scales, w1, w2_words, w2_scales, gate, offs, cen, pos1, pos2, pos3, out
):
    nc = tc.nc
    with ExitStack() as ctx:
        lists = ctx.enter_context(tc.tile_pool(name="lists", bufs=1))
        work = ctx.enter_context(tc.tile_pool(name="work", bufs=1))
        psum = ctx.enter_context(tc.psum_pool(name="psum", bufs=1))
        places = {"free": 0}

        def sbuf(shape, dtype, name, over=None, shift=0, room=0):
            if over is None:
                size = 4 if dtype in (F32, I32, U32) else 2 if dtype == BF16 else 1
                for extent in shape[1:]:
                    size = size * extent
                places[name] = places["free"]
                places["free"] = places["free"] + -(-max(size, room) // ALIGN) * ALIGN
            else:
                places[name] = places[over] + shift
            return work.tile(shape, dtype, name=name, align_bytes=ALIGN, offset=places[name])

        def reserve(name, size):
            places[name] = places["free"]
            places["free"] = places["free"] + size

        def bank(n, name):
            return psum.tile([P, BANK], F32, name=name, tag="bank%d" % n)

        def load_list(source, name):
            tile = lists.tile(list(source.shape), U16, name=name)
            nc.sync.dma_start(tile[:], source)
            return tile

        def load_words(z):
            tile = sbuf([P, T], I32, "x_window%d" % z)
            nc.sync.dma_start(out=tile[:], in_=x_words[z].rearrange("p n j -> p (n j)").bitcast(I32))
            return tile

        def load_w1(name, z, first, width, over=None, shift=0, room=0):
            tile = sbuf([P, PACK, width], F32, name, over, shift, room)
            rows = w1[z * P * PACK : (z + 1) * P * PACK, first : first + width]
            nc.sync.dma_start(out=tile[:], in_=rows.rearrange("(p j) c -> p j c", j=PACK))
            return tile

        raw_bytes = 4 * PACK * WIDE
        scale_window = sbuf([P, T], U8, "scale_window")
        nc.vector.memset(scale_window[QUAD : 2 * QUAD, :].bitcast(I32), 0)
        nc.vector.memset(scale_window[2 * QUAD : P, :].bitcast(I32), 0)
        x_plane = sbuf([P, S], U8, "x_plane")
        nc.vector.memset(x_plane[:].bitcast(I32), 0)
        gate_rows = sbuf([P, SPREAD, P], F32, "gate_rows")
        nc.gpsimd.memset(gate_rows[:], 0.0)
        warm = sbuf([P, 2], F32, "warm")
        nc.vector.memset(warm[:, 0:1], 0.0)
        nc.scalar.activation(out=warm[:, 1:2], in_=warm[:, 0:1], func=ACT.Silu)

        for z in range(PASSES):
            nc.sync.dma_start(
                out=scale_window[STRIPE * z : STRIPE * (z + 1), :].bitcast(I32),
                in_=x_scales[z].rearrange("(q r) n -> r q n", r=PACK).bitcast(I32),
            )
        offs_t = load_list(offs, "offs_t")
        nc.sync.dma_start(out=gate_rows[0:V_BLOCKS], in_=gate[0:SPREAD, 0, :].rearrange("d (c n) -> c d n", n=P))
        x_window = [load_words(0)]
        w1_raw = {(0, 0): load_w1("w1_raw0_0", 0, 0, P)[:]}
        x_window.append(load_words(1))
        w1_raw[0, 1] = load_w1("w1_raw0_1", 1, 0, P)[:]

        def pick(dst, window, a, b):
            nc.vector.tensor_copy(dst, window.indirect(offs_t[:, a // STRIPE : b // STRIPE]))

        picked_scales = sbuf([P, S], U8, "picked_scales")
        pick(picked_scales[:], scale_window[:], 0, S)
        for q in range(QUADS):
            nc.sync.dma_start(
                out=x_plane[QUAD * q : QUAD * q + PASSES * PACK, :].bitcast(I32),
                in_=picked_scales[q:QUAD:QUADS, 0:S].bitcast(I32),
            )

        rest = load_w1("w1_rest0", 0, P, H - P)
        w1_raw[1, 0] = rest[:, :, 0:P]
        w1_upper = [rest[:, :, P : H - P]]
        w1_raw[1, 1] = load_w1("w1_raw1_1", 1, P, P)[:]
        pos_t = [load_list(pos1, "pos_t0")]
        pos_t.append(load_list(pos2, "pos_t1"))
        w1_upper.append(load_w1("w1_upper1", 1, WIDE, WIDE)[:])
        pos_t.append(load_list(pos3, "pos_t2"))
        cen_t = load_list(cen, "cen_t")
        last_gate = sbuf([P, V], F32, "last_gate")
        nc.sync.dma_start(out=last_gate[:], in_=gate[SPREAD])
        w2_codes = sbuf([P, N], I32, "w2_codes")
        nc.sync.dma_start(out=w2_codes[:], in_=w2_words[0].rearrange("p n j -> p (n j)").bitcast(I32))
        w2_plane = sbuf([P, N], U8, "w2_plane")
        nc.gpsimd.memset(w2_plane[:].bitcast(I32), 0)
        for q in range(QUADS):
            nc.sync.dma_start(
                out=w2_plane[QUAD * q : QUAD * q + PACK, :].bitcast(I32),
                in_=w2_scales[0, PACK * q : PACK * (q + 1), :].bitcast(I32),
            )

        ident = sbuf([P, P], F32, "ident")
        make_identity(nc, ident[:])

        upright = bank(7, "gate_upright")
        for d in range(SPREAD):
            nc.tensor.transpose(upright[:, d * P : (d + 1) * P], gate_rows[:, d, :], ident[:])
        upright_columns = upright[:, 0 : SPREAD * P].rearrange("n (d c) -> n d c", d=SPREAD)
        columns = []
        for d in range(SPREAD):
            tile = sbuf([P, V_BLOCKS], F32, "gate_columns%d" % d, room=2 * P * PACK)
            nc.scalar.copy(out=tile[:], in_=upright_columns[:, d, 0:V_BLOCKS])
            columns.append(tile)
        spreads = []
        for d in range(SPREAD):
            spread = bank(d, "gate_spread")
            for c in range(V_BLOCKS):
                nc.tensor.transpose(
                    spread[:, c * P : (c + 1) * P], columns[d][:, c : c + 1].to_broadcast([P, P]), ident[:]
                )
            spreads.append(spread)
        gates = []
        for d in range(SPREAD):
            tile = sbuf([P, V], F32, "gate%d" % d)
            nc.scalar.copy(out=tile[:], in_=spreads[d][:])
            gates.append(tile)
        gates.append(last_gate)

        w1_mx = {}

        def quantize(grouped, width, name, room=0, over=None):
            codes = sbuf([P, width], U32, "codes_" + name, over, room=room)
            plane = sbuf([P, width], U8, "plane_" + name, room=room)
            nc.vector.quantize_mx(out=codes[:].bitcast(FP8X4), scales=plane[:], in_=grouped)
            return codes, plane

        def cast_tile(grouped, t, z, cast=nc.scalar.copy):
            cast(
                out=grouped.rearrange("p m e j -> p (m e) j").rearrange("p (c i) j -> p c j i", i=PACK),
                in_=w1_raw[t, z].rearrange("p j (c i) -> p c j i", i=PACK),
            )

        def staging(name, count, over=None, shift=0):
            return sbuf([P, count, HALF, 2, PACK], BF16, name, over, shift)

        def quantize_w1(grouped, keys, name, room=0, over=None):
            codes, plane = quantize(grouped.rearrange("p n m e j -> p (n m e j)"), len(keys) * P, name, room, over)
            for n, key in enumerate(keys):
                w1_mx[key] = (codes[:, n * P : (n + 1) * P], plane[:, n * P : (n + 1) * P])

        x_codes = [sbuf([P, S], U32, "x_codes0")]
        pick(x_codes[0][:], x_window[0][:].bitcast(U32), 0, S)
        first = staging("w1_bf0_0", 1)
        cast_tile(first[:, 0], 0, 0)
        quantize_w1(first[:], [(0, 0)], "w1_0_0")
        x_codes.append(sbuf([P, S - LAST], U32, "x_codes1"))
        for a, b in [(0, BANK), (BANK, S - LAST)]:
            pick(x_codes[1][:, a:b], x_window[1][:].bitcast(U32), a, b)
        second = staging("w1_bf0_1", 1, "gate_columns0")
        cast_tile(second[:, 0], 0, 1)
        quantize_w1(second[:], [(0, 1)], "w1_0_1", 4 * WIDE * PACK)
        x_last = sbuf([P, LAST], U32, "x_last", over="w1_raw0_1")
        pick(x_last[:], x_window[1][:].bitcast(U32), S - LAST, S)
        for z in range(PASSES):
            grouped = staging("w1_bf1_%d" % z, 1)
            cast_tile(grouped[:, 0], 1, z, nc.vector.tensor_copy)
            quantize_w1(grouped[:], [(1, z)], "w1_1_%d" % z)

        def picked_words(z, a, b):
            return x_last[:] if (z, a) == (1, S - LAST) else x_codes[z][:, a:b]

        def multiply(t, z, accs, cuts):
            codes, plane = w1_mx[t, z]
            for acc, (first, last) in zip(accs, cuts):
                stops = [first, S - LAST, last] if z == 1 and first < S - LAST < last else [first, last]
                for a, b in zip(stops, stops[1:]):
                    nc.tensor.matmul_mx(
                        out=acc[:, a - first : b - first],
                        lhsT=codes.bitcast(FP8X4),
                        lhsT_scale=plane,
                        rhs=picked_words(z, a, b).bitcast(FP8X4),
                        rhs_scale=x_plane[PACK * z : P, a:b],
                        start=(z == 0),
                        stop=(z == PASSES - 1 and b == last),
                    )

        h_tiles = {}

        def activate(t, accs, cuts, over=None):
            h = sbuf([P, S], F32, "h%d" % t, over)
            for acc, (first, last) in zip(accs, cuts):
                nc.scalar.activation(out=h[:, first:last], in_=acc[:, 0 : last - first], func=ACT.Silu)
            h_tiles[t] = h

        first_cuts = [(a, a + LAST) for a in range(0, S, LAST)]
        cuts = [(0, BANK), (BANK, S)]
        accs = {0: [bank(n, "acc0") for n in (2, 3, 4, 5)], 1: [bank(n, "acc1") for n in (6, 7)]}
        for z in range(PASSES):
            multiply(0, z, accs[0], first_cuts)
        activate(0, accs[0], first_cuts)
        for z in range(PASSES):
            multiply(1, z, accs[1], cuts)

        upper = staging("w1_bf_upper", 2 * PASSES, "codes_w1_0_1")

        def cast_upper(z):
            nc.scalar.copy(
                out=upper[:, 2 * z : 2 * z + 2].rearrange("p u m e j -> p m j u e"),
                in_=w1_upper[z].rearrange("p j (m u e) -> p m j u e", u=2, e=2),
            )

        cast_upper(0)
        activate(1, accs[1], cuts, "w1_rest0")
        accs[2] = [bank(n, "acc2") for n in (0, 1)]
        accs[3] = [bank(n, "acc3") for n in (2, 3)]

        def gather_gated(t, n, a, b, over=None, shift=0):
            term = sbuf([P, b - a], F32, "term%d_%d_%d" % (t, n, a), over, shift)
            offsets = pos_t[n][:, a // STRIPE : b // STRIPE]
            nc.vector.tensor_tensor(term[:], h_tiles[t][:].indirect(offsets), gates[n][:, a:b], MULT)
            return term

        def gather_plain(t, offsets, a, b, name, scale, over=None, shift=0, room=0):
            values = sbuf([P, b - a], F32, name, over, shift, room)
            nc.scalar.activation(
                out=values[:], in_=h_tiles[t][:].indirect(offsets[:, a // STRIPE : b // STRIPE]), func=ACT.Copy, scale=scale
            )
            return values

        def gate_plain(t, n, a, b, values):
            term = sbuf([P, b - a], F32, "term%d_%d_%d" % (t, n, a))
            nc.vector.tensor_tensor(term[:], values[:], gates[n][:, a:b], MULT)
            return term

        half_bytes = 4 * V
        mid = V // 2
        terms0 = [gather_gated(0, 0, 0, V, "w1_raw1_1"), gather_gated(0, 1, 0, V)]
        quantize_w1(upper[:, 0:1], [(2, 0)], "w1_2_0", over="codes_w1_1_1")
        multiply(2, 0, accs[2], cuts)
        terms1 = [gather_gated(1, 0, 0, V)]
        cast_upper(1)
        quantize_w1(upper[:, 1:], [(3, 0), (2, 1), (3, 1)], "w1_rest")
        for t, z in [(2, 1), (3, 0), (3, 1)]:
            multiply(t, z, accs[t], cuts)
        plain0 = gather_plain(0, pos_t[2], 0, V, "plain0", 1.0, room=4 * (mid + V))
        terms1.append(gather_gated(1, 1, 0, V, "w1_upper1", 0))
        terms0.append(gate_plain(0, 2, 0, V, plain0))
        terms1.append(gather_gated(1, 2, 0, V, "w1_upper1", half_bytes))
        halves = [gather_plain(0, cen_t, 0, mid, "own0_early", -1.0)]
        activate(2, accs[2], cuts)
        halves.append(gather_plain(0, cen_t, mid, V, "own0_late", -1.0, "plain0"))
        own = {1: gather_plain(1, cen_t, 0, V, "own1", -1.0, "plain0", 4 * mid)}
        activate(3, accs[3], cuts)
        for t in (2, 3):
            own[t] = gather_plain(t, cen_t, 0, V, "own%d" % t, -1.0)

        everyone, early, late = list(range(V_BLOCKS)), [0, 1], [2, 3]
        groups = [early, [2], [3]]
        z_bf = {group[0]: sbuf([P, len(group), 2, P, 2], BF16, "z_bf%d" % group[0]) for group in groups}

        def columns_of(tile, first, blocks):
            return [tile[:, vb * P - first : (vb + 1) * P - first] for vb in blocks]

        def sum_terms(parts, blocks, sum_bank):
            total = bank(sum_bank, "z_sum")
            for n, part in enumerate(parts):
                for i, piece in enumerate(part):
                    nc.tensor.matmul(
                        total[:, i * P : (i + 1) * P],
                        lhsT=piece,
                        rhs=ident[:],
                        is_transpose=True,
                        start=(n == 0 and i == 0),
                        stop=(n == len(parts) - 1 and i == len(blocks) - 1),
                    )
            return {vb: (total, i * P) for i, vb in enumerate(blocks)}

        def round_off(t, totals, blocks):
            total, at = totals[blocks[0]]
            sums = total[:, at : at + len(blocks) * P]
            rows = z_bf[blocks[0]]
            if t < 2:
                nc.scalar.copy(
                    out=rows[:, :, :, QUAD * t : QUAD * (t + 1), :],
                    in_=sums.rearrange("v (i m u e) -> v i u m e", m=QUAD, u=2, e=2),
                )
            else:
                nc.scalar.copy(out=rows[:, :, t - 2, HALF:P, :], in_=sums.rearrange("v (i m e) -> v i m e", m=HALF, e=2))

        def turn_back(turned, blocks, u):
            for i in range(len(blocks)):
                words = z_bf[blocks[0]][:, i, u].rearrange("v m e -> v (m e)").bitcast(F32)
                at = (u * len(blocks) + i) * P
                nc.tensor.transpose(turned[:, at : at + P], words, ident[:])

        def interleave(turned, blocks, move=nc.scalar.copy, over=None):
            width = len(blocks) * P
            grouped = sbuf([P, width, 2], F32, "z_grouped%d" % blocks[0], over)
            move(out=grouped[:], in_=turned[:, 0 : 2 * width].rearrange("m (u v) -> m v u", u=2))
            return grouped

        def quantize_z(grouped, blocks, over=None):
            words = grouped[:].rearrange("m v u -> m (v u)").bitcast(BF16)
            codes, plane = quantize(words, len(blocks) * P, "z%d" % blocks[0], over=over)
            return blocks[0] * P, codes, plane

        def project_out(group, out_bank, leave, result, first):
            start, codes, plane = group
            width = codes.shape[1]
            acc = bank(out_bank, "out_acc")
            nc.tensor.matmul_mx(
                out=acc[:, 0:width],
                lhsT=w2_codes[:].bitcast(FP8X4),
                lhsT_scale=w2_plane[:],
                rhs=codes[:].bitcast(FP8X4),
                rhs_scale=plane[:],
                start=True,
                stop=True,
            )
            leave(result[:, start - first : start - first + width], acc[:, 0:width], -1.0)

        first_own = columns_of(halves[0], 0, early) + columns_of(halves[1], mid, late)
        totals = [
            sum_terms([columns_of(x, 0, everyone) for x in terms0] + [first_own], everyone, 4),
            sum_terms([columns_of(x, 0, everyone) for x in terms1 + [own[1]]], everyone, 1),
        ]
        terms = [gather_gated(2, n, 0, V) for n in range(D)]
        totals.append(sum_terms([columns_of(x, 0, everyone) for x in terms + [own[2]]], everyone, 6))
        terms = [gather_gated(3, n, 0, mid) for n in range(D)]
        totals.append(sum_terms([columns_of(x, 0, early) for x in terms + [own[3]]], early, 7))
        turned = [bank(2, "turned")]
        for t in range(3):
            round_off(t, totals[t], early)
        turn_back(turned[0], early, 0)
        for t in (2, 0):
            for group in groups[1:]:
                round_off(t, totals[t], group)
        round_off(3, totals[3], early)
        turn_back(turned[0], early, 1)
        for group in groups[1:]:
            round_off(1, totals[1], group)
        last_totals = {}
        for vb, sum_bank in zip(late, (6, 7)):
            terms = [gather_gated(3, n, vb * P, (vb + 1) * P) for n in range(D)]
            last_totals[vb] = sum_terms([columns_of(own[3], 0, [vb])] + [[x[:]] for x in terms], [vb], sum_bank)
        turned += [bank(0, "turned"), bank(5, "turned")]
        for g in (1, 2):
            turn_back(turned[g], groups[g], 0)
        grouped = [interleave(turned[0], early, nc.vector.tensor_copy, "h3")]
        for g in (1, 2):
            round_off(3, last_totals[groups[g][0]], groups[g])
            turn_back(turned[g], groups[g], 1)
        grouped += [interleave(turned[g], groups[g]) for g in (1, 2)]
        results = [sbuf([P, 2 * P], F32, "result%d" % i) for i in range(2)]
        project_out(quantize_z(grouped[0], groups[0]), 3, nc.vector.tensor_scalar_mul, results[0], 0)
        nc.sync.dma_start(out=out[:, 0 : 2 * P], in_=results[0][:])
        project_out(quantize_z(grouped[1], groups[1]), 5, nc.scalar.mul, results[1], 2 * P)
        project_out(quantize_z(grouped[2], groups[2]), 4, nc.vector.tensor_scalar_mul, results[1], 2 * P)
        nc.sync.dma_start(out=out[:, 2 * P : V], in_=results[1][:])
